import numpy as np
import ml_dtypes


def mxq(x, axis, fmt="e4m3"):
    dtype, down = {"e4m3": (ml_dtypes.float8_e4m3fn, 7), "e5m2": (ml_dtypes.float8_e5m2, 14)}[fmt]
    v = np.moveaxis(np.asarray(x, np.float32).astype(ml_dtypes.bfloat16).astype(np.float64), axis, -1)
    blocks = v.reshape(v.shape[:-1] + (-1, 32))
    amax = np.abs(blocks).max(-1, keepdims=True)
    byte = np.maximum(np.where(amax > 0, np.frexp(amax)[1] - 1 + 127, 0) - down, 1)
    scale = np.exp2(byte - 127.0)
    codes = (blocks / scale).astype(np.float32).astype(dtype).astype(np.float64)
    return np.moveaxis((codes * scale).reshape(v.shape), -1, axis)


WIDE = False


def mx_kscale(k):
    if not WIDE:
        return np.ones(k)
    levels = np.array([10, -10, 5, -5, 0])
    if k % 512:
        return np.exp2(np.random.permutation(np.resize(levels, k // 32))).repeat(32)
    a = np.empty((k // 512, 16))
    for p in range(k // 512):
        a[p, :8] = np.random.permutation(np.resize(levels, 8))
        for g in range(8):
            far = levels[np.abs(levels - a[p, g]) >= 10]
            a[p, g + 8] = far[np.random.randint(len(far))]
    return np.exp2(a.ravel()).repeat(32)


def f64(x):
    return np.asarray(x).astype(np.float64)


def striped(idx):
    return np.tile(idx.reshape(-1, 16).T, (8, 1)).astype(np.uint16)


def unstriped(offs):
    return offs[:16].T.reshape(-1).astype(np.int64)


def pack_weight(w):
    k, n = w.shape
    w = f64(np.asarray(w, np.float32).astype(ml_dtypes.bfloat16)).reshape(k // 32, 32, n)
    amax = np.abs(w).max(1)
    byte = np.clip(np.where(amax > 0, np.frexp(amax)[1] - 1 + 127 - 7, 1), 1, 254)
    scaled = (w * np.exp2(127.0 - byte)[:, None, :]).reshape(k, n).astype(np.float32)
    words = np.ascontiguousarray(scaled.reshape(k // 512, 128, 4, n).transpose(0, 1, 3, 2)).astype(ml_dtypes.float8_e4m3fn).view(np.uint8)
    return words, np.ascontiguousarray(byte.astype(np.uint8).reshape(k // 512, 16, n))


def unpack_weight(words, scales):
    g, p, n, _ = words.shape
    vals = np.ascontiguousarray(words).view(ml_dtypes.float8_e4m3fn).astype(np.float64) * np.repeat(np.exp2(scales.astype(np.float64) - 127.0), 8, axis=1)[..., None]
    return vals.transpose(0, 1, 3, 2).reshape(g * 512, n)


K, T, S, V, H, N, D, W = 512, 1024, 512, 256, 512, 128, 2, 1024
P = 2 ** 7


def setup_inputs():
    n = np.random.standard_normal
    s = mx_kscale(K)[:, None]
    u = mx_kscale(H)
    near = np.random.permutation(S)
    packed_xT = pack_weight(n((K, T)) * s)
    packed_eT = pack_weight(n((K, W)) * s)
    return {
        "x_words": packed_xT[0],
        "x_scales": packed_xT[1],
        "e_words": packed_eT[0],
        "e_scales": packed_eT[1],
        "w1": (n((K, H)) / np.sqrt(K) / s * u).astype(np.float32),
        "w2": (n((K, H)) / np.sqrt(K) / s).astype(np.float32),
        "w3": (n((H, N)) / np.sqrt(2 * H) / u[:, None]).astype(np.float32),
        "w4": (n((H, N)) / np.sqrt(2 * H) / u[:, None]).astype(np.float32),
        "gate": (np.tile(np.random.uniform(0.3, 0.9, (D, 1, V)), (1, P, 1))).astype(np.float32),
        "offs": striped(np.random.permutation(T)[:S]),
        "usr": striped(np.random.permutation(W)[:V]),
        "pos1": striped(near[:V]),
        "pos2": striped(near[V:]),
    }


def reference(x_words, x_scales, e_words, e_scales, w1, w2, w3, w4, gate, offs, usr, pos1, pos2):
    xq = unpack_weight(x_words, x_scales)[:, unstriped(offs)]
    h = mxq(f64(w1), 0, "e4m3").T @ xq
    z = h[:, unstriped(pos1)] * f64(gate)[0, :1] + h[:, unstriped(pos2)] * f64(gate)[1, :1]
    e_usr = unpack_weight(e_words, e_scales)[:, unstriped(usr)]
    gg = mxq(f64(w2), 0, "e4m3").T @ e_usr
    y = z * gg
    return mxq(f64(w3), 0, "e4m3").T @ mxq(z, 0, "e4m3") + mxq(f64(w4), 0, "e4m3").T @ mxq(y, 0, "e4m3")

@@ -1,0 +1,170 @@
+from contextlib import ExitStack
+
+import concourse.mybir as mybir
+
+K, T, S, V, H, N = 512, 1024, 512, 256, 512, 128
+FLOPS = 2 * K * H * S + 2 * K * H * V + 2 * 2 * H * N * V
+
+F32 = mybir.dt.float32
+BF16 = mybir.dt.bfloat16
+I32 = mybir.dt.int32
+U32 = mybir.dt.uint32
+U16 = mybir.dt.uint16
+U8 = mybir.dt.uint8
+FP8X4 = mybir.dt.float8_e4m3fn_x4
+MULT = mybir.AluOpType.mult
+ADD = mybir.AluOpType.add
+
+P = 128
+PACK = 4
+HALF = V // 2
+
+
+def tile_picked_yngcf_none_p_kernel(
+    tc, x_words, x_scales, e_words, e_scales, w1, w2, w3, w4, gate, offs, usr, pos1, pos2, out
+):
+    nc = tc.nc
+    with ExitStack() as ctx:
+        sb = ctx.enter_context(tc.tile_pool(name="sb", bufs=1))
+        ps = ctx.enter_context(tc.psum_pool(name="ps", bufs=1))
+
+        def tile(name, shape, dtype):
+            return sb.tile(shape, dtype, name=name, align_bytes=64)
+
+        offs_sb = tile("offs_sb", [P, S // 16], U16)
+        usr_sb = tile("usr_sb", [P, V // 16], U16)
+        pos_sb = [tile(f"pos_sb{d}", [P, V // 16], U16) for d in range(2)]
+        xw_tab = tile("xw_tab", [P, T], I32)
+        ew_tab = tile("ew_tab", [P, T], I32)
+        xs_tab = tile("xs_tab", [P, T], U8)
+        es_tab = tile("es_tab", [P, T], U8)
+        w1_raw = [tile(f"w1_raw{c}", [P, PACK, H // 2], F32) for c in range(2)]
+        w2_raw = tile("w2_raw", [P, PACK, H], F32)
+        w3_raw = tile("w3_raw", [P, PACK, N], F32)
+        w4_raw = tile("w4_raw", [P, PACK, N], F32)
+        gate_sb = tile("gate_sb", [P, 2, V], F32)
+
+        def load_words(tab, words):
+            nc.sync.dma_start(out=tab[:], in_=words[0].rearrange("p n t -> p (n t)").bitcast(I32))
+
+        def load_scales(queue, tab, scales):
+            for q in range(4):
+                queue.dma_start(
+                    out=tab[32 * q : 32 * q + 4, :].bitcast(I32),
+                    in_=scales[0, 4 * q : 4 * q + 4, :].bitcast(I32),
+                )
+
+        nc.vector.memset(xs_tab[:].bitcast(I32), 0)
+        nc.gpsimd.memset(es_tab[:].bitcast(I32), 0)
+        nc.sync.dma_start(offs_sb[:], offs)
+        load_words(xw_tab, x_words)
+        load_scales(nc.scalar, xs_tab, x_scales)
+        load_scales(nc.gpsimd, es_tab, e_scales)
+        w1_rows = w1.rearrange("(p j) c -> p j c", j=PACK)
+        for c in range(2):
+            nc.sync.dma_start(out=w1_raw[c][:], in_=w1_rows[:, :, c * (H // 2) : (c + 1) * (H // 2)])
+        load_words(ew_tab, e_words)
+        nc.sync.dma_start(out=gate_sb[:], in_=gate.rearrange("d p v -> p d v"))
+        nc.sync.dma_start(usr_sb[:], usr)
+        nc.sync.dma_start(pos_sb[0][:], pos1)
+        nc.sync.dma_start(pos_sb[1][:], pos2)
+        nc.sync.dma_start(out=w2_raw[:], in_=w2.rearrange("(p j) c -> p j c", j=PACK))
+        nc.sync.dma_start(out=w3_raw[:], in_=w3.rearrange("(p j) c -> p j c", j=PACK))
+        nc.sync.dma_start(out=w4_raw[:], in_=w4.rearrange("(p j) c -> p j c", j=PACK))
+
+        x_codes = tile("x_codes", [P, S], U32)
+        x_sc = tile("x_sc", [P, S], U8)
+        nc.vector.tensor_copy(x_codes[:], xw_tab[:].bitcast(U32).indirect(offs_sb[:]))
+        nc.vector.tensor_copy(x_sc[:], xs_tab[:].indirect(offs_sb[:]))
+
+        def deal(copy, grouped, raw, m0, m1, raw_m0):
+            copy(
+                out=grouped[:].rearrange("p t (m j) -> p m j t", j=PACK)[:, m0:m1],
+                in_=raw[:].rearrange("p j (m t) -> p m j t", t=PACK)[:, m0 - raw_m0 : m1 - raw_m0],
+            )
+
+        w1_bf = tile("w1_bf", [P, PACK, P * PACK], BF16)
+        deal(nc.scalar.copy, w1_bf, w1_raw[0], 0, 64, 0)
+        deal(nc.scalar.copy, w1_bf, w1_raw[1], 64, 84, 64)
+        deal(nc.vector.tensor_copy, w1_bf, w1_raw[1], 84, 128, 64)
+
+        w1_codes = tile("w1_codes", [P, PACK, P], U32)
+        w1_sc = tile("w1_sc", [P, PACK, P], U8)
+        h_sb = [tile(f"h_sb{t}", [P, S], F32) for t in range(PACK)]
+        for t in range(PACK):
+            nc.vector.quantize_mx(out=w1_codes[:, t, :].bitcast(FP8X4), scales=w1_sc[:, t, :], in_=w1_bf[:, t, :])
+            h_ps = ps.tile([P, S], F32, name=f"h_ps{t}")
+            nc.tensor.matmul_mx(
+                out=h_ps[:], lhsT=w1_codes[:, t, :].bitcast(FP8X4), lhsT_scale=w1_sc[:, t, :],
+                rhs=x_codes[:].bitcast(FP8X4), rhs_scale=x_sc[:], start=True, stop=True,
+            )
+            nc.scalar.copy(out=h_sb[t][:], in_=h_ps[:])
+
+        e_codes = tile("e_codes", [P, V], U32)
+        e_sc = tile("e_sc", [P, V], U8)
+        nc.vector.tensor_copy(e_codes[:], ew_tab[:].bitcast(U32).indirect(usr_sb[:]))
+        nc.vector.tensor_copy(e_sc[:], es_tab[:].indirect(usr_sb[:]))
+
+        w2_bf = tile("w2_bf", [P, PACK, P * PACK], BF16)
+        deal(nc.scalar.copy, w2_bf, w2_raw, 0, 128, 0)
+        w34_bf = tile("w34_bf", [P, 2, N * PACK], BF16)
+        for s, raw in enumerate((w3_raw, w4_raw)):
+            nc.scalar.copy(
+                out=w34_bf[:, s, :].rearrange("p (c i j) -> p c j i", i=4, j=PACK),
+                in_=raw[:].rearrange("p j (c i) -> p c j i", i=4),
+            )
+
+        terms = [tile(f"term{d}", [P, PACK, V], F32) for d in range(2)]
+        z = tile("z", [P, PACK, V], F32)
+        w2_codes = tile("w2_codes", [P, H], U32)
+        w2_sc = tile("w2_sc", [P, H], U8)
+        w34_codes = tile("w34_codes", [P, 2 * N], U32)
+        w34_sc = tile("w34_sc", [P, 2 * N], U8)
+        for t in range(PACK):
+            for d in range(2):
+                nc.vector.tensor_tensor(terms[d][:, t, :], h_sb[t][:].indirect(pos_sb[d][:]), gate_sb[:, d, :], MULT)
+            if t == 2:
+                nc.vector.quantize_mx(
+                    out=w2_codes[:].bitcast(FP8X4), scales=w2_sc[:], in_=w2_bf[:].rearrange("p t c -> p (t c)")
+                )
+        nc.vector.tensor_tensor(z[:, 0:3, :], terms[0][:, 0:3, :], terms[1][:, 0:3, :], ADD)
+        nc.vector.tensor_tensor(z[:, 3, :], terms[0][:, 3, :], terms[1][:, 3, :], ADD)
+        nc.vector.quantize_mx(
+            out=w34_codes[:].bitcast(FP8X4), scales=w34_sc[:], in_=w34_bf[:].rearrange("p s c -> p (s c)")
+        )
+
+        gg_ps = [ps.tile([P, PACK, HALF], F32, name=f"gg_ps{u}") for u in range(2)]
+        for u in range(2):
+            for t in range(PACK):
+                nc.tensor.matmul_mx(
+                    out=gg_ps[u][:, t, :], lhsT=w2_codes[:, t * P : (t + 1) * P].bitcast(FP8X4),
+                    lhsT_scale=w2_sc[:, t * P : (t + 1) * P],
+                    rhs=e_codes[:, u * HALF : (u + 1) * HALF].bitcast(FP8X4),
+                    rhs_scale=e_sc[:, u * HALF : (u + 1) * HALF], start=True, stop=True,
+                )
+
+        zy_bf = [tile(f"zy_bf{u}", [P, 2, HALF * PACK], BF16) for u in range(2)]
+        for u in range(2):
+            z_walk = z[:, :, u * HALF : (u + 1) * HALF].rearrange("p t (c i) -> p c t i", i=4)
+            nc.scalar.copy(out=zy_bf[u][:, 0, :].rearrange("p (c i t) -> p c t i", i=4, t=PACK), in_=z_walk)
+            nc.vector.tensor_tensor(
+                zy_bf[u][:, 1, :].rearrange("p (c i t) -> p c t i", i=4, t=PACK),
+                gg_ps[u][:].rearrange("p t (c i) -> p c t i", i=4), z_walk, MULT,
+            )
+        for u in range(2):
+            zy_codes = tile(f"zy_codes{u}", [P, 2 * HALF], U32)
+            zy_sc = tile(f"zy_sc{u}", [P, 2 * HALF], U8)
+            nc.vector.quantize_mx(
+                out=zy_codes[:].bitcast(FP8X4), scales=zy_sc[:], in_=zy_bf[u][:].rearrange("p s c -> p (s c)")
+            )
+            out_ps = ps.tile([P, HALF], F32, name=f"out_ps{u}")
+            for s in range(2):
+                nc.tensor.matmul_mx(
+                    out=out_ps[:], lhsT=w34_codes[:, s * N : (s + 1) * N].bitcast(FP8X4),
+                    lhsT_scale=w34_sc[:, s * N : (s + 1) * N],
+                    rhs=zy_codes[:, s * HALF : (s + 1) * HALF].bitcast(FP8X4),
+                    rhs_scale=zy_sc[:, s * HALF : (s + 1) * HALF], start=(s == 0), stop=(s == 1),
+                )
+            out_sb = tile(f"out_sb{u}", [P, HALF], F32)
+            nc.scalar.copy(out=out_sb[:], in_=out_ps[:])
+            nc.sync.dma_start(out=out[:, u * HALF : (u + 1) * HALF], in_=out_sb[:])

@@ -28,21 +28,20 @@ def tile_picked_yngcf_none_p_kernel(
         sb = ctx.enter_context(tc.tile_pool(name="sb", bufs=1))
         ps = ctx.enter_context(tc.psum_pool(name="ps", bufs=1))
 
-        def tile(name, shape, dtype):
-            return sb.tile(shape, dtype, name=name, align_bytes=64)
+        def tile(name, shape, dtype, tag=None):
+            return sb.tile(shape, dtype, name=name, tag=tag or name, align_bytes=64)
 
         offs_sb = tile("offs_sb", [P, S // 16], U16)
         usr_sb = tile("usr_sb", [P, V // 16], U16)
         pos_sb = [tile(f"pos_sb{d}", [P, V // 16], U16) for d in range(2)]
         xw_tab = tile("xw_tab", [P, T], I32)
         ew_tab = tile("ew_tab", [P, T], I32)
+        gate_sb = tile("gate_sb", [P, 2, V], F32)
+        w2_raw = tile("w2_raw", [P, PACK, H], F32)
+        w34_raw = tile("w34_raw", [P, 2, PACK, N], F32)
         xs_tab = tile("xs_tab", [P, T], U8)
         es_tab = tile("es_tab", [P, T], U8)
         w1_raw = [tile(f"w1_raw{c}", [P, PACK, H // 2], F32) for c in range(2)]
-        w2_raw = tile("w2_raw", [P, PACK, H], F32)
-        w3_raw = tile("w3_raw", [P, PACK, N], F32)
-        w4_raw = tile("w4_raw", [P, PACK, N], F32)
-        gate_sb = tile("gate_sb", [P, 2, V], F32)
 
         def load_words(tab, words):
             nc.sync.dma_start(out=tab[:], in_=words[0].rearrange("p n t -> p (n t)").bitcast(I32))
@@ -54,23 +53,26 @@ def tile_picked_yngcf_none_p_kernel(
                     in_=scales[0, 4 * q : 4 * q + 4, :].bitcast(I32),
                 )
 
-        nc.vector.memset(xs_tab[:].bitcast(I32), 0)
+        def load_halves(raw, w):
+            rows = w.rearrange("(p j) c -> p j c", j=PACK)
+            for c in range(2):
+                nc.sync.dma_start(out=raw[c][:], in_=rows[:, :, c * (H // 2) : (c + 1) * (H // 2)])
+
+        nc.gpsimd.memset(xs_tab[:].bitcast(I32), 0)
         nc.gpsimd.memset(es_tab[:].bitcast(I32), 0)
         nc.sync.dma_start(offs_sb[:], offs)
-        load_words(xw_tab, x_words)
-        load_scales(nc.scalar, xs_tab, x_scales)
-        load_scales(nc.gpsimd, es_tab, e_scales)
-        w1_rows = w1.rearrange("(p j) c -> p j c", j=PACK)
-        for c in range(2):
-            nc.sync.dma_start(out=w1_raw[c][:], in_=w1_rows[:, :, c * (H // 2) : (c + 1) * (H // 2)])
-        load_words(ew_tab, e_words)
-        nc.sync.dma_start(out=gate_sb[:], in_=gate.rearrange("d p v -> p d v"))
         nc.sync.dma_start(usr_sb[:], usr)
         nc.sync.dma_start(pos_sb[0][:], pos1)
+        load_words(xw_tab, x_words)
         nc.sync.dma_start(pos_sb[1][:], pos2)
+        load_scales(nc.sync, xs_tab, x_scales)
+        load_halves(w1_raw, w1)
+        load_words(ew_tab, e_words)
+        nc.sync.dma_start(out=gate_sb[:], in_=gate.rearrange("d p v -> p d v"))
+        load_scales(nc.sync, es_tab, e_scales)
         nc.sync.dma_start(out=w2_raw[:], in_=w2.rearrange("(p j) c -> p j c", j=PACK))
-        nc.sync.dma_start(out=w3_raw[:], in_=w3.rearrange("(p j) c -> p j c", j=PACK))
-        nc.sync.dma_start(out=w4_raw[:], in_=w4.rearrange("(p j) c -> p j c", j=PACK))
+        for s, w in enumerate((w3, w4)):
+            nc.sync.dma_start(out=w34_raw[:, s], in_=w.rearrange("(p j) c -> p j c", j=PACK))
 
         x_codes = tile("x_codes", [P, S], U32)
         x_sc = tile("x_sc", [P, S], U8)
@@ -83,10 +85,9 @@ def tile_picked_yngcf_none_p_kernel(
                 in_=raw[:].rearrange("p j (m t) -> p m j t", t=PACK)[:, m0 - raw_m0 : m1 - raw_m0],
             )
 
-        w1_bf = tile("w1_bf", [P, PACK, P * PACK], BF16)
+        w1_bf = tile("w1_bf", [P, PACK, P * PACK], BF16, "w1bf_ecodes")
         deal(nc.scalar.copy, w1_bf, w1_raw[0], 0, 64, 0)
-        deal(nc.scalar.copy, w1_bf, w1_raw[1], 64, 84, 64)
-        deal(nc.vector.tensor_copy, w1_bf, w1_raw[1], 84, 128, 64)
+        deal(nc.scalar.copy, w1_bf, w1_raw[1], 64, 128, 64)
 
         w1_codes = tile("w1_codes", [P, PACK, P], U32)
         w1_sc = tile("w1_sc", [P, PACK, P], U8)
@@ -100,35 +101,37 @@ def tile_picked_yngcf_none_p_kernel(
             )
             nc.scalar.copy(out=h_sb[t][:], in_=h_ps[:])
 
-        e_codes = tile("e_codes", [P, V], U32)
+        e_codes = tile("e_codes", [P, V], U32, "w1bf_ecodes")
         e_sc = tile("e_sc", [P, V], U8)
         nc.vector.tensor_copy(e_codes[:], ew_tab[:].bitcast(U32).indirect(usr_sb[:]))
         nc.vector.tensor_copy(e_sc[:], es_tab[:].indirect(usr_sb[:]))
 
-        w2_bf = tile("w2_bf", [P, PACK, P * PACK], BF16)
+        w2_bf = tile("w2_bf", [P, PACK, P * PACK], BF16, "w2bf_term")
         deal(nc.scalar.copy, w2_bf, w2_raw, 0, 128, 0)
         w34_bf = tile("w34_bf", [P, 2, N * PACK], BF16)
-        for s, raw in enumerate((w3_raw, w4_raw)):
+        for s in range(2):
             nc.scalar.copy(
                 out=w34_bf[:, s, :].rearrange("p (c i j) -> p c j i", i=4, j=PACK),
-                in_=raw[:].rearrange("p j (c i) -> p c j i", i=4),
+                in_=w34_raw[:, s].rearrange("p j (c i) -> p c j i", i=4),
             )
 
-        terms = [tile(f"term{d}", [P, PACK, V], F32) for d in range(2)]
+        terms = [tile(f"term{d}", [P, PACK - 1, V], F32) for d in range(2)]
         z = tile("z", [P, PACK, V], F32)
         w2_codes = tile("w2_codes", [P, H], U32)
         w2_sc = tile("w2_sc", [P, H], U8)
         w34_codes = tile("w34_codes", [P, 2 * N], U32)
         w34_sc = tile("w34_sc", [P, 2 * N], U8)
-        for t in range(PACK):
+        for t in range(PACK - 1):
             for d in range(2):
                 nc.vector.tensor_tensor(terms[d][:, t, :], h_sb[t][:].indirect(pos_sb[d][:]), gate_sb[:, d, :], MULT)
-            if t == 2:
-                nc.vector.quantize_mx(
-                    out=w2_codes[:].bitcast(FP8X4), scales=w2_sc[:], in_=w2_bf[:].rearrange("p t c -> p (t c)")
-                )
-        nc.vector.tensor_tensor(z[:, 0:3, :], terms[0][:, 0:3, :], terms[1][:, 0:3, :], ADD)
-        nc.vector.tensor_tensor(z[:, 3, :], terms[0][:, 3, :], terms[1][:, 3, :], ADD)
+        nc.vector.tensor_tensor(z[:, 0:3, :], terms[0][:], terms[1][:], ADD)
+        nc.vector.quantize_mx(
+            out=w2_codes[:].bitcast(FP8X4), scales=w2_sc[:], in_=w2_bf[:].rearrange("p t c -> p (t c)")
+        )
+        last = tile("last", [P, 2, V], F32, "w2bf_term")
+        for d in range(2):
+            nc.vector.tensor_tensor(last[:, d, :], h_sb[3][:].indirect(pos_sb[d][:]), gate_sb[:, d, :], MULT)
+        nc.vector.tensor_tensor(z[:, 3, :], last[:, 0, :], last[:, 1, :], ADD)
         nc.vector.quantize_mx(
             out=w34_codes[:].bitcast(FP8X4), scales=w34_sc[:], in_=w34_bf[:].rearrange("p s c -> p (s c)")
         )

@@ -79,35 +79,43 @@ def tile_picked_yngcf_none_p_kernel(
         nc.vector.tensor_copy(x_codes[:], xw_tab[:].bitcast(U32).indirect(offs_sb[:]))
         nc.vector.tensor_copy(x_sc[:], xs_tab[:].indirect(offs_sb[:]))
 
-        def deal(copy, grouped, raw, m0, m1, raw_m0):
-            copy(
-                out=grouped[:].rearrange("p t (m j) -> p m j t", j=PACK)[:, m0:m1],
-                in_=raw[:].rearrange("p j (m t) -> p m j t", t=PACK)[:, m0 - raw_m0 : m1 - raw_m0],
+        def deal(grouped, raw, m0, t0):
+            n_t, n_m = grouped.shape[1], raw.shape[2] // PACK
+            nc.scalar.copy(
+                out=grouped[:].rearrange("p t (m j) -> p m j t", j=PACK)[:, m0 : m0 + n_m],
+                in_=raw[:].rearrange("p j (m t) -> p m j t", t=PACK)[:, :, :, t0 : t0 + n_t],
             )
 
-        w1_bf = tile("w1_bf", [P, PACK, P * PACK], BF16, "w1bf_ecodes")
-        deal(nc.scalar.copy, w1_bf, w1_raw[0], 0, 64, 0)
-        deal(nc.scalar.copy, w1_bf, w1_raw[1], 64, 128, 64)
+        w1_bf = [tile(f"w1_bf{a}", [P, 2, P * PACK], BF16, f"w1bf{a}") for a in range(2)]
+        for c in range(2):
+            for a in range(2):
+                deal(w1_bf[a], w1_raw[c], 64 * c, 2 * a)
 
-        w1_codes = tile("w1_codes", [P, PACK, P], U32)
-        w1_sc = tile("w1_sc", [P, PACK, P], U8)
+        w1_codes = tile("w1_codes", [P, H], U32)
+        w1_sc = tile("w1_sc", [P, H], U8)
+
+        def quantize(codes, scales, values):
+            nc.vector.quantize_mx(out=codes.bitcast(FP8X4), scales=scales, in_=values)
+
+        quantize(w1_codes[:, 0:P], w1_sc[:, 0:P], w1_bf[0][:, 0, :])
+        quantize(w1_codes[:, P : 2 * P], w1_sc[:, P : 2 * P], w1_bf[0][:, 1, :])
+        quantize(w1_codes[:, 2 * P :], w1_sc[:, 2 * P :], w1_bf[1][:].rearrange("p t c -> p (t c)"))
         h_sb = [tile(f"h_sb{t}", [P, S], F32) for t in range(PACK)]
         for t in range(PACK):
-            nc.vector.quantize_mx(out=w1_codes[:, t, :].bitcast(FP8X4), scales=w1_sc[:, t, :], in_=w1_bf[:, t, :])
             h_ps = ps.tile([P, S], F32, name=f"h_ps{t}")
             nc.tensor.matmul_mx(
-                out=h_ps[:], lhsT=w1_codes[:, t, :].bitcast(FP8X4), lhsT_scale=w1_sc[:, t, :],
+                out=h_ps[:], lhsT=w1_codes[:, t * P : (t + 1) * P].bitcast(FP8X4), lhsT_scale=w1_sc[:, t * P : (t + 1) * P],
                 rhs=x_codes[:].bitcast(FP8X4), rhs_scale=x_sc[:], start=True, stop=True,
             )
             nc.scalar.copy(out=h_sb[t][:], in_=h_ps[:])
 
-        e_codes = tile("e_codes", [P, V], U32, "w1bf_ecodes")
+        e_codes = tile("e_codes", [P, V], U32, "w1bf0")
         e_sc = tile("e_sc", [P, V], U8)
         nc.vector.tensor_copy(e_codes[:], ew_tab[:].bitcast(U32).indirect(usr_sb[:]))
         nc.vector.tensor_copy(e_sc[:], es_tab[:].indirect(usr_sb[:]))
 
         w2_bf = tile("w2_bf", [P, PACK, P * PACK], BF16, "w2bf_term")
-        deal(nc.scalar.copy, w2_bf, w2_raw, 0, 128, 0)
+        deal(w2_bf, w2_raw, 0, 0)
         w34_bf = tile("w34_bf", [P, 2, N * PACK], BF16)
         for s in range(2):
             nc.scalar.copy(
@@ -115,26 +123,16 @@ def tile_picked_yngcf_none_p_kernel(
                 in_=w34_raw[:, s].rearrange("p j (c i) -> p c j i", i=4),
             )
 
-        terms = [tile(f"term{d}", [P, PACK - 1, V], F32) for d in range(2)]
-        z = tile("z", [P, PACK, V], F32)
         w2_codes = tile("w2_codes", [P, H], U32)
         w2_sc = tile("w2_sc", [P, H], U8)
         w34_codes = tile("w34_codes", [P, 2 * N], U32)
         w34_sc = tile("w34_sc", [P, 2 * N], U8)
-        for t in range(PACK - 1):
+        terms = [tile(f"term{d}", [P, PACK, V], F32) for d in range(2)]
+        for t in range(PACK):
             for d in range(2):
                 nc.vector.tensor_tensor(terms[d][:, t, :], h_sb[t][:].indirect(pos_sb[d][:]), gate_sb[:, d, :], MULT)
-        nc.vector.tensor_tensor(z[:, 0:3, :], terms[0][:], terms[1][:], ADD)
-        nc.vector.quantize_mx(
-            out=w2_codes[:].bitcast(FP8X4), scales=w2_sc[:], in_=w2_bf[:].rearrange("p t c -> p (t c)")
-        )
-        last = tile("last", [P, 2, V], F32, "w2bf_term")
-        for d in range(2):
-            nc.vector.tensor_tensor(last[:, d, :], h_sb[3][:].indirect(pos_sb[d][:]), gate_sb[:, d, :], MULT)
-        nc.vector.tensor_tensor(z[:, 3, :], last[:, 0, :], last[:, 1, :], ADD)
-        nc.vector.quantize_mx(
-            out=w34_codes[:].bitcast(FP8X4), scales=w34_sc[:], in_=w34_bf[:].rearrange("p s c -> p (s c)")
-        )
+        quantize(w2_codes[:], w2_sc[:], w2_bf[:].rearrange("p t c -> p (t c)"))
+        quantize(w34_codes[:], w34_sc[:], w34_bf[:].rearrange("p s c -> p (s c)"))
 
         gg_ps = [ps.tile([P, PACK, HALF], F32, name=f"gg_ps{u}") for u in range(2)]
         for u in range(2):
@@ -146,28 +144,30 @@ def tile_picked_yngcf_none_p_kernel(
                     rhs_scale=e_sc[:, u * HALF : (u + 1) * HALF], start=True, stop=True,
                 )
 
+        z = [tile(f"z{u}", [P, HALF * PACK], F32, ("w2bf_term", None)[u]) for u in range(2)]
         zy_bf = [tile(f"zy_bf{u}", [P, 2, HALF * PACK], BF16) for u in range(2)]
         for u in range(2):
-            z_walk = z[:, :, u * HALF : (u + 1) * HALF].rearrange("p t (c i) -> p c t i", i=4)
-            nc.scalar.copy(out=zy_bf[u][:, 0, :].rearrange("p (c i t) -> p c t i", i=4, t=PACK), in_=z_walk)
+            a, b = (term[:, :, u * HALF : (u + 1) * HALF].rearrange("p t (c i) -> p c t i", i=4) for term in terms)
+            nc.vector.tensor_tensor(z[u][:].rearrange("p (c i t) -> p c t i", i=4, t=PACK), a, b, ADD)
+            nc.scalar.copy(out=zy_bf[u][:, 0, :], in_=z[u][:])
+        for u in range(2):
             nc.vector.tensor_tensor(
-                zy_bf[u][:, 1, :].rearrange("p (c i t) -> p c t i", i=4, t=PACK),
-                gg_ps[u][:].rearrange("p t (c i) -> p c t i", i=4), z_walk, MULT,
+                zy_bf[u][:, 1, :].rearrange("p (v t) -> p v t", t=PACK),
+                gg_ps[u][:].rearrange("p t v -> p v t"),
+                z[u][:].rearrange("p (v t) -> p v t", t=PACK), MULT,
             )
         for u in range(2):
             zy_codes = tile(f"zy_codes{u}", [P, 2 * HALF], U32)
             zy_sc = tile(f"zy_sc{u}", [P, 2 * HALF], U8)
-            nc.vector.quantize_mx(
-                out=zy_codes[:].bitcast(FP8X4), scales=zy_sc[:], in_=zy_bf[u][:].rearrange("p s c -> p (s c)")
-            )
             out_ps = ps.tile([P, HALF], F32, name=f"out_ps{u}")
             for s in range(2):
+                cols = slice(s * HALF, (s + 1) * HALF)
+                quantize(zy_codes[:, cols], zy_sc[:, cols], zy_bf[u][:, s, :])
                 nc.tensor.matmul_mx(
                     out=out_ps[:], lhsT=w34_codes[:, s * N : (s + 1) * N].bitcast(FP8X4),
                     lhsT_scale=w34_sc[:, s * N : (s + 1) * N],
-                    rhs=zy_codes[:, s * HALF : (s + 1) * HALF].bitcast(FP8X4),
-                    rhs_scale=zy_sc[:, s * HALF : (s + 1) * HALF], start=(s == 0), stop=(s == 1),
+                    rhs=zy_codes[:, cols].bitcast(FP8X4), rhs_scale=zy_sc[:, cols], start=(s == 0), stop=(s == 1),
                 )
             out_sb = tile(f"out_sb{u}", [P, HALF], F32)
             nc.scalar.copy(out=out_sb[:], in_=out_ps[:])
-            nc.sync.dma_start(out=out[:, u * HALF : (u + 1) * HALF], in_=out_sb[:])
+            (nc.sync, nc.scalar)[u].dma_start(out=out[:, u * HALF : (u + 1) * HALF], in_=out_sb[:])

@@ -40,7 +40,7 @@ def tile_picked_yngcf_none_p_kernel(
         w2_raw = tile("w2_raw", [P, PACK, H], F32)
         w34_raw = tile("w34_raw", [P, 2, PACK, N], F32)
         xs_tab = tile("xs_tab", [P, T], U8)
-        es_tab = tile("es_tab", [P, T], U8)
+        es_tab = tile("es_tab", [P, T], U8, "es_term")
         w1_raw = [tile(f"w1_raw{c}", [P, PACK, H // 2], F32) for c in range(2)]
 
         def load_words(tab, words):
@@ -59,7 +59,7 @@ def tile_picked_yngcf_none_p_kernel(
                 nc.sync.dma_start(out=raw[c][:], in_=rows[:, :, c * (H // 2) : (c + 1) * (H // 2)])
 
         nc.gpsimd.memset(xs_tab[:].bitcast(I32), 0)
-        nc.gpsimd.memset(es_tab[:].bitcast(I32), 0)
+        nc.vector.memset(es_tab[:].bitcast(I32), 0)
         nc.sync.dma_start(offs_sb[:], offs)
         nc.sync.dma_start(usr_sb[:], usr)
         nc.sync.dma_start(pos_sb[0][:], pos1)
@@ -101,13 +101,14 @@ def tile_picked_yngcf_none_p_kernel(
         quantize(w1_codes[:, P : 2 * P], w1_sc[:, P : 2 * P], w1_bf[0][:, 1, :])
         quantize(w1_codes[:, 2 * P :], w1_sc[:, 2 * P :], w1_bf[1][:].rearrange("p t c -> p (t c)"))
         h_sb = [tile(f"h_sb{t}", [P, S], F32) for t in range(PACK)]
-        for t in range(PACK):
-            h_ps = ps.tile([P, S], F32, name=f"h_ps{t}")
+        pieces = [(0, 0, S // 2), (0, S // 2, S)] + [(t, 0, S) for t in range(1, PACK)]
+        for b, (t, j0, j1) in enumerate(pieces):
+            h_ps = ps.tile([P, j1 - j0], F32, name=f"h_ps{b}", tag=f"bank{b}")
             nc.tensor.matmul_mx(
                 out=h_ps[:], lhsT=w1_codes[:, t * P : (t + 1) * P].bitcast(FP8X4), lhsT_scale=w1_sc[:, t * P : (t + 1) * P],
-                rhs=x_codes[:].bitcast(FP8X4), rhs_scale=x_sc[:], start=True, stop=True,
+                rhs=x_codes[:, j0:j1].bitcast(FP8X4), rhs_scale=x_sc[:, j0:j1], start=True, stop=True,
             )
-            nc.scalar.copy(out=h_sb[t][:], in_=h_ps[:])
+            nc.scalar.copy(out=h_sb[t][:, j0:j1], in_=h_ps[:])
 
         e_codes = tile("e_codes", [P, V], U32, "w1bf0")
         e_sc = tile("e_sc", [P, V], U8)
@@ -127,7 +128,8 @@ def tile_picked_yngcf_none_p_kernel(
         w2_sc = tile("w2_sc", [P, H], U8)
         w34_codes = tile("w34_codes", [P, 2 * N], U32)
         w34_sc = tile("w34_sc", [P, 2 * N], U8)
-        terms = [tile(f"term{d}", [P, PACK, V], F32) for d in range(2)]
+        both_terms = tile("both_terms", [P, 2, PACK, V], F32, "es_term")
+        terms = [both_terms[:, d] for d in range(2)]
         for t in range(PACK):
             for d in range(2):
                 nc.vector.tensor_tensor(terms[d][:, t, :], h_sb[t][:].indirect(pos_sb[d][:]), gate_sb[:, d, :], MULT)
@@ -144,22 +146,22 @@ def tile_picked_yngcf_none_p_kernel(
                     rhs_scale=e_sc[:, u * HALF : (u + 1) * HALF], start=True, stop=True,
                 )
 
-        z = [tile(f"z{u}", [P, HALF * PACK], F32, ("w2bf_term", None)[u]) for u in range(2)]
+        z = [tile(f"z{u}", [P, PACK, HALF], F32, ("w2bf_term", None)[u]) for u in range(2)]
         zy_bf = [tile(f"zy_bf{u}", [P, 2, HALF * PACK], BF16) for u in range(2)]
+        z_walk = [z[u][:].rearrange("p t (c i) -> p c t i", i=4) for u in range(2)]
         for u in range(2):
-            a, b = (term[:, :, u * HALF : (u + 1) * HALF].rearrange("p t (c i) -> p c t i", i=4) for term in terms)
-            nc.vector.tensor_tensor(z[u][:].rearrange("p (c i t) -> p c t i", i=4, t=PACK), a, b, ADD)
-            nc.scalar.copy(out=zy_bf[u][:, 0, :], in_=z[u][:])
+            users = slice(u * HALF, (u + 1) * HALF)
+            nc.vector.tensor_tensor(z[u][:], terms[0][:, :, users], terms[1][:, :, users], ADD)
+            nc.scalar.copy(out=zy_bf[u][:, 0, :].rearrange("p (c i t) -> p c t i", i=4, t=PACK), in_=z_walk[u])
         for u in range(2):
             nc.vector.tensor_tensor(
-                zy_bf[u][:, 1, :].rearrange("p (v t) -> p v t", t=PACK),
-                gg_ps[u][:].rearrange("p t v -> p v t"),
-                z[u][:].rearrange("p (v t) -> p v t", t=PACK), MULT,
+                zy_bf[u][:, 1, :].rearrange("p (c i t) -> p c t i", i=4, t=PACK),
+                gg_ps[u][:].rearrange("p t (c i) -> p c t i", i=4), z_walk[u], MULT,
             )
         for u in range(2):
             zy_codes = tile(f"zy_codes{u}", [P, 2 * HALF], U32)
             zy_sc = tile(f"zy_sc{u}", [P, 2 * HALF], U8)
-            out_ps = ps.tile([P, HALF], F32, name=f"out_ps{u}")
+            out_ps = ps.tile([P, HALF], F32, name=f"out_ps{u}", tag=f"bank{u}")
             for s in range(2):
                 cols = slice(s * HALF, (s + 1) * HALF)
                 quantize(zy_codes[:, cols], zy_sc[:, cols], zy_bf[u][:, s, :])

@@ -1,6 +1,7 @@
 from contextlib import ExitStack
 
 import concourse.mybir as mybir
+from concourse.masks import make_identity
 
 K, T, S, V, H, N = 512, 1024, 512, 256, 512, 128
 FLOPS = 2 * K * H * S + 2 * K * H * V + 2 * 2 * H * N * V
@@ -14,6 +15,7 @@ U8 = mybir.dt.uint8
 FP8X4 = mybir.dt.float8_e4m3fn_x4
 MULT = mybir.AluOpType.mult
 ADD = mybir.AluOpType.add
+COPY = mybir.ActivationFunctionType.Copy
 
 P = 128
 PACK = 4
@@ -60,6 +62,8 @@ def tile_picked_yngcf_none_p_kernel(
 
         nc.gpsimd.memset(xs_tab[:].bitcast(I32), 0)
         nc.vector.memset(es_tab[:].bitcast(I32), 0)
+        ident = tile("ident", [P, P], F32)
+        make_identity(nc, ident[:])
         nc.sync.dma_start(offs_sb[:], offs)
         nc.sync.dma_start(usr_sb[:], usr)
         nc.sync.dma_start(pos_sb[0][:], pos1)
@@ -115,6 +119,29 @@ def tile_picked_yngcf_none_p_kernel(
         nc.vector.tensor_copy(e_codes[:], ew_tab[:].bitcast(U32).indirect(usr_sb[:]))
         nc.vector.tensor_copy(e_sc[:], es_tab[:].indirect(usr_sb[:]))
 
+        both_terms = tile("both_terms", [P, 2, PACK, V], F32, "es_term")
+        terms = [both_terms[:, d] for d in range(2)]
+        gate_ps = ps.tile([P, 4, P], F32, name="gate_ps", tag="bank3")
+        for d in range(2):
+            for u in range(2):
+                nc.tensor.transpose(gate_ps[:, 2 * d + u, :], gate_sb[:, d, u * HALF : (u + 1) * HALF], ident[:])
+        gate_col = tile("gate_col", [P, 4], F32)
+        nc.scalar.copy(out=gate_col[:], in_=gate_ps[:, :, 0])
+        turned = ps.tile([P, 4, P], F32, name="turned", tag="bank4")
+        gated = tile("gated", [P, 4, P], F32)
+        for d in range(2):
+            nc.vector.tensor_copy(terms[d][:, 0, :], h_sb[0][:].indirect(pos_sb[d][:]))
+            for u in range(2):
+                nc.tensor.transpose(turned[:, 2 * d + u, :], terms[d][:, 0, u * HALF : (u + 1) * HALF], ident[:])
+        for a in range(4):
+            nc.scalar.activation(out=gated[:, a, :], in_=turned[:, a, :], func=COPY, scale=gate_col[:, a : a + 1])
+        z_ps = ps.tile([P, 2, HALF], F32, name="z_ps", tag="bank2")
+        for u in range(2):
+            for d in range(2):
+                nc.tensor.matmul(
+                    z_ps[:, u, :], gated[:, 2 * d + u, :], ident[:], start=(d == 0), stop=(d == 1), is_transpose=True
+                )
+
         w2_bf = tile("w2_bf", [P, PACK, P * PACK], BF16, "w2bf_term")
         deal(w2_bf, w2_raw, 0, 0)
         w34_bf = tile("w34_bf", [P, 2, N * PACK], BF16)
@@ -128,9 +155,7 @@ def tile_picked_yngcf_none_p_kernel(
         w2_sc = tile("w2_sc", [P, H], U8)
         w34_codes = tile("w34_codes", [P, 2 * N], U32)
         w34_sc = tile("w34_sc", [P, 2 * N], U8)
-        both_terms = tile("both_terms", [P, 2, PACK, V], F32, "es_term")
-        terms = [both_terms[:, d] for d in range(2)]
-        for t in range(PACK):
+        for t in range(1, PACK):
             for d in range(2):
                 nc.vector.tensor_tensor(terms[d][:, t, :], h_sb[t][:].indirect(pos_sb[d][:]), gate_sb[:, d, :], MULT)
         quantize(w2_codes[:], w2_sc[:], w2_bf[:].rearrange("p t c -> p (t c)"))
@@ -146,12 +171,14 @@ def tile_picked_yngcf_none_p_kernel(
                     rhs_scale=e_sc[:, u * HALF : (u + 1) * HALF], start=True, stop=True,
                 )
 
-        z = [tile(f"z{u}", [P, PACK, HALF], F32, ("w2bf_term", None)[u]) for u in range(2)]
+        z_all = tile("z_all", [P, 2, PACK, HALF], F32, "w2bf_term")
+        nc.scalar.copy(out=z_all[:, :, 0, :], in_=z_ps[:])
+        z = [z_all[:, u] for u in range(2)]
         zy_bf = [tile(f"zy_bf{u}", [P, 2, HALF * PACK], BF16) for u in range(2)]
-        z_walk = [z[u][:].rearrange("p t (c i) -> p c t i", i=4) for u in range(2)]
+        z_walk = [z[u].rearrange("p t (c i) -> p c t i", i=4) for u in range(2)]
         for u in range(2):
             users = slice(u * HALF, (u + 1) * HALF)
-            nc.vector.tensor_tensor(z[u][:], terms[0][:, :, users], terms[1][:, :, users], ADD)
+            nc.vector.tensor_tensor(z[u][:, 1:, :], terms[0][:, 1:, users], terms[1][:, 1:, users], ADD)
             nc.scalar.copy(out=zy_bf[u][:, 0, :].rearrange("p (c i t) -> p c t i", i=4, t=PACK), in_=z_walk[u])
         for u in range(2):
             nc.vector.tensor_tensor(

@@ -1,7 +1,6 @@
 from contextlib import ExitStack
 
 import concourse.mybir as mybir
-from concourse.masks import make_identity
 
 K, T, S, V, H, N = 512, 1024, 512, 256, 512, 128
 FLOPS = 2 * K * H * S + 2 * K * H * V + 2 * 2 * H * N * V
@@ -15,7 +14,6 @@ U8 = mybir.dt.uint8
 FP8X4 = mybir.dt.float8_e4m3fn_x4
 MULT = mybir.AluOpType.mult
 ADD = mybir.AluOpType.add
-COPY = mybir.ActivationFunctionType.Copy
 
 P = 128
 PACK = 4
@@ -42,58 +40,51 @@ def tile_picked_yngcf_none_p_kernel(
         w2_raw = tile("w2_raw", [P, PACK, H], F32)
         w34_raw = tile("w34_raw", [P, 2, PACK, N], F32)
         xs_tab = tile("xs_tab", [P, T], U8)
-        es_tab = tile("es_tab", [P, T], U8, "es_term")
+        es_tab = tile("es_tab", [P, T], U8, "es_w2codes")
         w1_raw = [tile(f"w1_raw{c}", [P, PACK, H // 2], F32) for c in range(2)]
 
         def load_words(tab, words):
             nc.sync.dma_start(out=tab[:], in_=words[0].rearrange("p n t -> p (n t)").bitcast(I32))
 
-        def load_scales(queue, tab, scales):
+        def load_scales(queues, tab, scales):
             for q in range(4):
-                queue.dma_start(
-                    out=tab[32 * q : 32 * q + 4, :].bitcast(I32),
-                    in_=scales[0, 4 * q : 4 * q + 4, :].bitcast(I32),
+                queues[q % len(queues)].dma_start(
+                    out=tab[32 * q : 32 * q + 32, :].bitcast(I32),
+                    in_=scales[0, 4 * q : 4 * q + 4, :].bitcast(I32).partition_broadcast(8),
                 )
 
-        def load_halves(raw, w):
-            rows = w.rearrange("(p j) c -> p j c", j=PACK)
-            for c in range(2):
-                nc.sync.dma_start(out=raw[c][:], in_=rows[:, :, c * (H // 2) : (c + 1) * (H // 2)])
-
-        nc.gpsimd.memset(xs_tab[:].bitcast(I32), 0)
-        nc.vector.memset(es_tab[:].bitcast(I32), 0)
-        ident = tile("ident", [P, P], F32)
-        make_identity(nc, ident[:])
         nc.sync.dma_start(offs_sb[:], offs)
+        load_scales((nc.scalar, nc.sync), xs_tab, x_scales)
+        load_words(xw_tab, x_words)
+        w1_rows = w1.rearrange("(p j) c -> p j c", j=PACK)
+        for c in range(2):
+            nc.sync.dma_start(out=w1_raw[c][:], in_=w1_rows[:, :, c * (H // 2) : (c + 1) * (H // 2)])
         nc.sync.dma_start(usr_sb[:], usr)
         nc.sync.dma_start(pos_sb[0][:], pos1)
-        load_words(xw_tab, x_words)
         nc.sync.dma_start(pos_sb[1][:], pos2)
-        load_scales(nc.sync, xs_tab, x_scales)
-        load_halves(w1_raw, w1)
         load_words(ew_tab, e_words)
         nc.sync.dma_start(out=gate_sb[:], in_=gate.rearrange("d p v -> p d v"))
-        load_scales(nc.sync, es_tab, e_scales)
         nc.sync.dma_start(out=w2_raw[:], in_=w2.rearrange("(p j) c -> p j c", j=PACK))
+        load_scales((nc.sync,), es_tab, e_scales)
         for s, w in enumerate((w3, w4)):
             nc.sync.dma_start(out=w34_raw[:, s], in_=w.rearrange("(p j) c -> p j c", j=PACK))
 
         x_codes = tile("x_codes", [P, S], U32)
         x_sc = tile("x_sc", [P, S], U8)
-        nc.vector.tensor_copy(x_codes[:], xw_tab[:].bitcast(U32).indirect(offs_sb[:]))
         nc.vector.tensor_copy(x_sc[:], xs_tab[:].indirect(offs_sb[:]))
+        nc.vector.tensor_copy(x_codes[:], xw_tab[:].bitcast(U32).indirect(offs_sb[:]))
 
-        def deal(grouped, raw, m0, t0):
+        def deal(copy, grouped, raw, m0, t0):
             n_t, n_m = grouped.shape[1], raw.shape[2] // PACK
-            nc.scalar.copy(
+            copy(
                 out=grouped[:].rearrange("p t (m j) -> p m j t", j=PACK)[:, m0 : m0 + n_m],
                 in_=raw[:].rearrange("p j (m t) -> p m j t", t=PACK)[:, :, :, t0 : t0 + n_t],
             )
 
         w1_bf = [tile(f"w1_bf{a}", [P, 2, P * PACK], BF16, f"w1bf{a}") for a in range(2)]
         for c in range(2):
-            for a in range(2):
-                deal(w1_bf[a], w1_raw[c], 64 * c, 2 * a)
+            deal(nc.vector.tensor_copy, w1_bf[0], w1_raw[c], 64 * c, 0)
+            deal(nc.scalar.copy, w1_bf[1], w1_raw[c], 64 * c, 2)
 
         w1_codes = tile("w1_codes", [P, H], U32)
         w1_sc = tile("w1_sc", [P, H], U8)
@@ -119,31 +110,11 @@ def tile_picked_yngcf_none_p_kernel(
         nc.vector.tensor_copy(e_codes[:], ew_tab[:].bitcast(U32).indirect(usr_sb[:]))
         nc.vector.tensor_copy(e_sc[:], es_tab[:].indirect(usr_sb[:]))
 
-        both_terms = tile("both_terms", [P, 2, PACK, V], F32, "es_term")
+        both_terms = tile("both_terms", [P, 2, PACK, V], F32)
         terms = [both_terms[:, d] for d in range(2)]
-        gate_ps = ps.tile([P, 4, P], F32, name="gate_ps", tag="bank3")
-        for d in range(2):
-            for u in range(2):
-                nc.tensor.transpose(gate_ps[:, 2 * d + u, :], gate_sb[:, d, u * HALF : (u + 1) * HALF], ident[:])
-        gate_col = tile("gate_col", [P, 4], F32)
-        nc.scalar.copy(out=gate_col[:], in_=gate_ps[:, :, 0])
-        turned = ps.tile([P, 4, P], F32, name="turned", tag="bank4")
-        gated = tile("gated", [P, 4, P], F32)
-        for d in range(2):
-            nc.vector.tensor_copy(terms[d][:, 0, :], h_sb[0][:].indirect(pos_sb[d][:]))
-            for u in range(2):
-                nc.tensor.transpose(turned[:, 2 * d + u, :], terms[d][:, 0, u * HALF : (u + 1) * HALF], ident[:])
-        for a in range(4):
-            nc.scalar.activation(out=gated[:, a, :], in_=turned[:, a, :], func=COPY, scale=gate_col[:, a : a + 1])
-        z_ps = ps.tile([P, 2, HALF], F32, name="z_ps", tag="bank2")
-        for u in range(2):
-            for d in range(2):
-                nc.tensor.matmul(
-                    z_ps[:, u, :], gated[:, 2 * d + u, :], ident[:], start=(d == 0), stop=(d == 1), is_transpose=True
-                )
 
         w2_bf = tile("w2_bf", [P, PACK, P * PACK], BF16, "w2bf_term")
-        deal(w2_bf, w2_raw, 0, 0)
+        deal(nc.scalar.copy, w2_bf, w2_raw, 0, 0)
         w34_bf = tile("w34_bf", [P, 2, N * PACK], BF16)
         for s in range(2):
             nc.scalar.copy(
@@ -151,11 +122,11 @@ def tile_picked_yngcf_none_p_kernel(
                 in_=w34_raw[:, s].rearrange("p j (c i) -> p c j i", i=4),
             )
 
-        w2_codes = tile("w2_codes", [P, H], U32)
+        w2_codes = tile("w2_codes", [P, H], U32, "es_w2codes")
         w2_sc = tile("w2_sc", [P, H], U8)
         w34_codes = tile("w34_codes", [P, 2 * N], U32)
         w34_sc = tile("w34_sc", [P, 2 * N], U8)
-        for t in range(1, PACK):
+        for t in range(PACK):
             for d in range(2):
                 nc.vector.tensor_tensor(terms[d][:, t, :], h_sb[t][:].indirect(pos_sb[d][:]), gate_sb[:, d, :], MULT)
         quantize(w2_codes[:], w2_sc[:], w2_bf[:].rearrange("p t c -> p (t c)"))
@@ -172,13 +143,12 @@ def tile_picked_yngcf_none_p_kernel(
                 )
 
         z_all = tile("z_all", [P, 2, PACK, HALF], F32, "w2bf_term")
-        nc.scalar.copy(out=z_all[:, :, 0, :], in_=z_ps[:])
         z = [z_all[:, u] for u in range(2)]
         zy_bf = [tile(f"zy_bf{u}", [P, 2, HALF * PACK], BF16) for u in range(2)]
         z_walk = [z[u].rearrange("p t (c i) -> p c t i", i=4) for u in range(2)]
         for u in range(2):
             users = slice(u * HALF, (u + 1) * HALF)
-            nc.vector.tensor_tensor(z[u][:, 1:, :], terms[0][:, 1:, users], terms[1][:, 1:, users], ADD)
+            nc.vector.tensor_tensor(z[u], terms[0][:, :, users], terms[1][:, :, users], ADD)
             nc.scalar.copy(out=zy_bf[u][:, 0, :].rearrange("p (c i t) -> p c t i", i=4, t=PACK), in_=z_walk[u])
         for u in range(2):
             nc.vector.tensor_tensor(

@@ -46,26 +46,35 @@ def tile_picked_yngcf_none_p_kernel(
         def load_words(tab, words):
             nc.sync.dma_start(out=tab[:], in_=words[0].rearrange("p n t -> p (n t)").bitcast(I32))
 
-        def load_scales(queues, tab, scales):
+        def load_scales(tab, scales):
             for q in range(4):
-                queues[q % len(queues)].dma_start(
-                    out=tab[32 * q : 32 * q + 32, :].bitcast(I32),
-                    in_=scales[0, 4 * q : 4 * q + 4, :].bitcast(I32).partition_broadcast(8),
+                nc.sync.dma_start(
+                    out=tab[32 * q : 32 * q + 4, :].bitcast(I32),
+                    in_=scales[0, 4 * q : 4 * q + 4, :].bitcast(I32),
                 )
 
-        nc.sync.dma_start(offs_sb[:], offs)
-        load_scales((nc.scalar, nc.sync), xs_tab, x_scales)
-        load_words(xw_tab, x_words)
+        nc.gpsimd.memset(es_tab[:].bitcast(I32), 0)
         w1_rows = w1.rearrange("(p j) c -> p j c", j=PACK)
-        for c in range(2):
+
+        def load_w1(c):
             nc.sync.dma_start(out=w1_raw[c][:], in_=w1_rows[:, :, c * (H // 2) : (c + 1) * (H // 2)])
+
+        nc.sync.dma_start(offs_sb[:], offs)
+        for q in range(4):
+            (nc.scalar, nc.sync)[q % 2].dma_start(
+                out=xs_tab[32 * q : 32 * q + 32, :].bitcast(I32),
+                in_=x_scales[0, 4 * q : 4 * q + 4, :].bitcast(I32).partition_broadcast(8),
+            )
+        load_words(xw_tab, x_words)
+        load_w1(0)
+        load_w1(1)
         nc.sync.dma_start(usr_sb[:], usr)
         nc.sync.dma_start(pos_sb[0][:], pos1)
         nc.sync.dma_start(pos_sb[1][:], pos2)
         load_words(ew_tab, e_words)
         nc.sync.dma_start(out=gate_sb[:], in_=gate.rearrange("d p v -> p d v"))
         nc.sync.dma_start(out=w2_raw[:], in_=w2.rearrange("(p j) c -> p j c", j=PACK))
-        load_scales((nc.sync,), es_tab, e_scales)
+        load_scales(es_tab, e_scales)
         for s, w in enumerate((w3, w4)):
             nc.sync.dma_start(out=w34_raw[:, s], in_=w.rearrange("(p j) c -> p j c", j=PACK))
 
@@ -82,9 +91,10 @@ def tile_picked_yngcf_none_p_kernel(
             )
 
         w1_bf = [tile(f"w1_bf{a}", [P, 2, P * PACK], BF16, f"w1bf{a}") for a in range(2)]
-        for c in range(2):
-            deal(nc.vector.tensor_copy, w1_bf[0], w1_raw[c], 64 * c, 0)
-            deal(nc.scalar.copy, w1_bf[1], w1_raw[c], 64 * c, 2)
+        deal(nc.vector.tensor_copy, w1_bf[0], w1_raw[0], 0, 0)
+        deal(nc.scalar.copy, w1_bf[1], w1_raw[0], 0, 2)
+        deal(nc.vector.tensor_copy, w1_bf[0], w1_raw[1], 64, 0)
+        deal(nc.scalar.copy, w1_bf[1], w1_raw[1], 64, 2)
 
         w1_codes = tile("w1_codes", [P, H], U32)
         w1_sc = tile("w1_sc", [P, H], U8)
@@ -110,7 +120,7 @@ def tile_picked_yngcf_none_p_kernel(
         nc.vector.tensor_copy(e_codes[:], ew_tab[:].bitcast(U32).indirect(usr_sb[:]))
         nc.vector.tensor_copy(e_sc[:], es_tab[:].indirect(usr_sb[:]))
 
-        both_terms = tile("both_terms", [P, 2, PACK, V], F32)
+        both_terms = tile("both_terms", [P, 2, PACK, V], F32, "terms_w34codes")
         terms = [both_terms[:, d] for d in range(2)]
 
         w2_bf = tile("w2_bf", [P, PACK, P * PACK], BF16, "w2bf_term")
@@ -124,13 +134,10 @@ def tile_picked_yngcf_none_p_kernel(
 
         w2_codes = tile("w2_codes", [P, H], U32, "es_w2codes")
         w2_sc = tile("w2_sc", [P, H], U8)
-        w34_codes = tile("w34_codes", [P, 2 * N], U32)
-        w34_sc = tile("w34_sc", [P, 2 * N], U8)
         for t in range(PACK):
             for d in range(2):
                 nc.vector.tensor_tensor(terms[d][:, t, :], h_sb[t][:].indirect(pos_sb[d][:]), gate_sb[:, d, :], MULT)
         quantize(w2_codes[:], w2_sc[:], w2_bf[:].rearrange("p t c -> p (t c)"))
-        quantize(w34_codes[:], w34_sc[:], w34_bf[:].rearrange("p s c -> p (s c)"))
 
         gg_ps = [ps.tile([P, PACK, HALF], F32, name=f"gg_ps{u}") for u in range(2)]
         for u in range(2):
@@ -150,6 +157,9 @@ def tile_picked_yngcf_none_p_kernel(
             users = slice(u * HALF, (u + 1) * HALF)
             nc.vector.tensor_tensor(z[u], terms[0][:, :, users], terms[1][:, :, users], ADD)
             nc.scalar.copy(out=zy_bf[u][:, 0, :].rearrange("p (c i t) -> p c t i", i=4, t=PACK), in_=z_walk[u])
+        w34_codes = tile("w34_codes", [P, 2 * N], U32, "terms_w34codes")
+        w34_sc = tile("w34_sc", [P, 2 * N], U8)
+        quantize(w34_codes[:], w34_sc[:], w34_bf[:].rearrange("p s c -> p (s c)"))
         for u in range(2):
             nc.vector.tensor_tensor(
                 zy_bf[u][:, 1, :].rearrange("p (c i t) -> p c t i", i=4, t=PACK),

@@ -40,8 +40,9 @@ def tile_picked_yngcf_none_p_kernel(
         w2_raw = tile("w2_raw", [P, PACK, H], F32)
         w34_raw = tile("w34_raw", [P, 2, PACK, N], F32)
         xs_tab = tile("xs_tab", [P, T], U8)
-        es_tab = tile("es_tab", [P, T], U8, "es_w2codes")
-        w1_raw = [tile(f"w1_raw{c}", [P, PACK, H // 2], F32) for c in range(2)]
+        es_tab = tile("es_tab", [P, T], U8, "terms_w34codes")
+        w1_cuts = (0, 3 * H // 4, H)
+        w1_raw = [tile(f"w1_raw{c}", [P, PACK, w1_cuts[c + 1] - w1_cuts[c]], F32) for c in range(2)]
 
         def load_words(tab, words):
             nc.sync.dma_start(out=tab[:], in_=words[0].rearrange("p n t -> p (n t)").bitcast(I32))
@@ -57,7 +58,7 @@ def tile_picked_yngcf_none_p_kernel(
         w1_rows = w1.rearrange("(p j) c -> p j c", j=PACK)
 
         def load_w1(c):
-            nc.sync.dma_start(out=w1_raw[c][:], in_=w1_rows[:, :, c * (H // 2) : (c + 1) * (H // 2)])
+            nc.sync.dma_start(out=w1_raw[c][:], in_=w1_rows[:, :, w1_cuts[c] : w1_cuts[c + 1]])
 
         nc.sync.dma_start(offs_sb[:], offs)
         for q in range(4):
@@ -69,12 +70,12 @@ def tile_picked_yngcf_none_p_kernel(
         load_w1(0)
         load_w1(1)
         nc.sync.dma_start(usr_sb[:], usr)
-        nc.sync.dma_start(pos_sb[0][:], pos1)
-        nc.sync.dma_start(pos_sb[1][:], pos2)
+        load_scales(es_tab, e_scales)
         load_words(ew_tab, e_words)
         nc.sync.dma_start(out=gate_sb[:], in_=gate.rearrange("d p v -> p d v"))
+        nc.sync.dma_start(pos_sb[0][:], pos1)
+        nc.sync.dma_start(pos_sb[1][:], pos2)
         nc.sync.dma_start(out=w2_raw[:], in_=w2.rearrange("(p j) c -> p j c", j=PACK))
-        load_scales(es_tab, e_scales)
         for s, w in enumerate((w3, w4)):
             nc.sync.dma_start(out=w34_raw[:, s], in_=w.rearrange("(p j) c -> p j c", j=PACK))
 
@@ -93,8 +94,8 @@ def tile_picked_yngcf_none_p_kernel(
         w1_bf = [tile(f"w1_bf{a}", [P, 2, P * PACK], BF16, f"w1bf{a}") for a in range(2)]
         deal(nc.vector.tensor_copy, w1_bf[0], w1_raw[0], 0, 0)
         deal(nc.scalar.copy, w1_bf[1], w1_raw[0], 0, 2)
-        deal(nc.vector.tensor_copy, w1_bf[0], w1_raw[1], 64, 0)
-        deal(nc.scalar.copy, w1_bf[1], w1_raw[1], 64, 2)
+        deal(nc.vector.tensor_copy, w1_bf[0], w1_raw[1], w1_cuts[1] // PACK, 0)
+        deal(nc.scalar.copy, w1_bf[1], w1_raw[1], w1_cuts[1] // PACK, 2)
 
         w1_codes = tile("w1_codes", [P, H], U32)
         w1_sc = tile("w1_sc", [P, H], U8)
@@ -132,7 +133,7 @@ def tile_picked_yngcf_none_p_kernel(
                 in_=w34_raw[:, s].rearrange("p j (c i) -> p c j i", i=4),
             )
 
-        w2_codes = tile("w2_codes", [P, H], U32, "es_w2codes")
+        w2_codes = tile("w2_codes", [P, H], U32)
         w2_sc = tile("w2_sc", [P, H], U8)
         for t in range(PACK):
             for d in range(2):

@@ -1,6 +1,7 @@
 from contextlib import ExitStack
 
 import concourse.mybir as mybir
+from concourse.masks import make_identity
 
 K, T, S, V, H, N = 512, 1024, 512, 256, 512, 128
 FLOPS = 2 * K * H * S + 2 * K * H * V + 2 * 2 * H * N * V
@@ -14,6 +15,7 @@ U8 = mybir.dt.uint8
 FP8X4 = mybir.dt.float8_e4m3fn_x4
 MULT = mybir.AluOpType.mult
 ADD = mybir.AluOpType.add
+COPY = mybir.ActivationFunctionType.Copy
 
 P = 128
 PACK = 4
@@ -31,34 +33,31 @@ def tile_picked_yngcf_none_p_kernel(
         def tile(name, shape, dtype, tag=None):
             return sb.tile(shape, dtype, name=name, tag=tag or name, align_bytes=64)
 
+        def bank(name, shape, b):
+            return ps.tile(shape, F32, name=name, tag=f"bank{b}")
+
         offs_sb = tile("offs_sb", [P, S // 16], U16)
         usr_sb = tile("usr_sb", [P, V // 16], U16)
         pos_sb = [tile(f"pos_sb{d}", [P, V // 16], U16) for d in range(2)]
         xw_tab = tile("xw_tab", [P, T], I32)
         ew_tab = tile("ew_tab", [P, T], I32)
-        gate_sb = tile("gate_sb", [P, 2, V], F32)
-        w2_raw = tile("w2_raw", [P, PACK, H], F32)
-        w34_raw = tile("w34_raw", [P, 2, PACK, N], F32)
+        gate_col = tile("gate_col", [P, 4], F32)
+        gate_sb = [tile(f"gate_sb{d}", [P, V], F32) for d in range(2)]
+        w2_raw = [tile(f"w2_raw{c}", [P, PACK, H // 2], F32) for c in range(2)]
+        w34_raw = [tile(f"w34_raw{s}", [P, PACK, N], F32) for s in range(2)]
         xs_tab = tile("xs_tab", [P, T], U8)
-        es_tab = tile("es_tab", [P, T], U8, "terms_w34codes")
-        w1_cuts = (0, 3 * H // 4, H)
+        es_tab = tile("es_tab", [P, T], U8)
+        w1_cuts = (0, 5 * H // 8, H)
         w1_raw = [tile(f"w1_raw{c}", [P, PACK, w1_cuts[c + 1] - w1_cuts[c]], F32) for c in range(2)]
+        ident = tile("ident", [P, P], F32)
 
         def load_words(tab, words):
             nc.sync.dma_start(out=tab[:], in_=words[0].rearrange("p n t -> p (n t)").bitcast(I32))
 
-        def load_scales(tab, scales):
-            for q in range(4):
-                nc.sync.dma_start(
-                    out=tab[32 * q : 32 * q + 4, :].bitcast(I32),
-                    in_=scales[0, 4 * q : 4 * q + 4, :].bitcast(I32),
-                )
-
         nc.gpsimd.memset(es_tab[:].bitcast(I32), 0)
+        make_identity(nc, ident[:])
         w1_rows = w1.rearrange("(p j) c -> p j c", j=PACK)
-
-        def load_w1(c):
-            nc.sync.dma_start(out=w1_raw[c][:], in_=w1_rows[:, :, w1_cuts[c] : w1_cuts[c + 1]])
+        w2_rows = w2.rearrange("(p j) c -> p j c", j=PACK)
 
         nc.sync.dma_start(offs_sb[:], offs)
         for q in range(4):
@@ -67,80 +66,114 @@ def tile_picked_yngcf_none_p_kernel(
                 in_=x_scales[0, 4 * q : 4 * q + 4, :].bitcast(I32).partition_broadcast(8),
             )
         load_words(xw_tab, x_words)
-        load_w1(0)
-        load_w1(1)
+        for c in range(2):
+            nc.sync.dma_start(out=w1_raw[c][:], in_=w1_rows[:, :, w1_cuts[c] : w1_cuts[c + 1]])
         nc.sync.dma_start(usr_sb[:], usr)
-        load_scales(es_tab, e_scales)
+        for q in range(4):
+            nc.sync.dma_start(
+                out=es_tab[32 * q : 32 * q + 4, :].bitcast(I32), in_=e_scales[0, 4 * q : 4 * q + 4, :].bitcast(I32)
+            )
         load_words(ew_tab, e_words)
-        nc.sync.dma_start(out=gate_sb[:], in_=gate.rearrange("d p v -> p d v"))
+        nc.sync.dma_start(out=w2_raw[0][:], in_=w2_rows[:, :, : H // 2])
         nc.sync.dma_start(pos_sb[0][:], pos1)
         nc.sync.dma_start(pos_sb[1][:], pos2)
-        nc.sync.dma_start(out=w2_raw[:], in_=w2.rearrange("(p j) c -> p j c", j=PACK))
+        nc.sync.dma_start(out=w2_raw[1][:], in_=w2_rows[:, :, H // 2 :])
+        gate_rows = gate.rearrange("d p (u v) -> (d p u) v", u=2)
+        with nc.allow_non_contiguous_dma(reason="one gate value a partition"):
+            nc.sync.dma_start(out=gate_col[:], in_=gate_rows[0:388:129, :].rearrange("n v -> v n"))
+        for d in range(2):
+            nc.sync.dma_start(out=gate_sb[d][:], in_=gate[d])
         for s, w in enumerate((w3, w4)):
-            nc.sync.dma_start(out=w34_raw[:, s], in_=w.rearrange("(p j) c -> p j c", j=PACK))
+            rows = w.rearrange("(b a x) c -> a b (x c)", a=2, x=16)
+            for a in range(2):
+                nc.sync.dma_start(out=w34_raw[s][:, 2 * a : 2 * a + 2].rearrange("p e c -> p (e c)"), in_=rows[a])
 
         x_codes = tile("x_codes", [P, S], U32)
         x_sc = tile("x_sc", [P, S], U8)
         nc.vector.tensor_copy(x_sc[:], xs_tab[:].indirect(offs_sb[:]))
         nc.vector.tensor_copy(x_codes[:], xw_tab[:].bitcast(U32).indirect(offs_sb[:]))
 
-        def deal(copy, grouped, raw, m0, t0):
-            n_t, n_m = grouped.shape[1], raw.shape[2] // PACK
+        def deal(copy, grouped, raw, b0, a):
+            n_b = raw.shape[2] // 32
             copy(
-                out=grouped[:].rearrange("p t (m j) -> p m j t", j=PACK)[:, m0 : m0 + n_m],
-                in_=raw[:].rearrange("p j (m t) -> p m j t", t=PACK)[:, :, :, t0 : t0 + n_t],
+                out=grouped.rearrange("p e (b r j) -> p b r j e", r=8, j=PACK)[:, b0 : b0 + n_b],
+                in_=raw[:].rearrange("p j (b a r e) -> p a b r j e", a=2, r=8, e=2)[:, a],
             )
-
-        w1_bf = [tile(f"w1_bf{a}", [P, 2, P * PACK], BF16, f"w1bf{a}") for a in range(2)]
-        deal(nc.vector.tensor_copy, w1_bf[0], w1_raw[0], 0, 0)
-        deal(nc.scalar.copy, w1_bf[1], w1_raw[0], 0, 2)
-        deal(nc.vector.tensor_copy, w1_bf[0], w1_raw[1], w1_cuts[1] // PACK, 0)
-        deal(nc.scalar.copy, w1_bf[1], w1_raw[1], w1_cuts[1] // PACK, 2)
-
-        w1_codes = tile("w1_codes", [P, H], U32)
-        w1_sc = tile("w1_sc", [P, H], U8)
 
         def quantize(codes, scales, values):
             nc.vector.quantize_mx(out=codes.bitcast(FP8X4), scales=scales, in_=values)
 
-        quantize(w1_codes[:, 0:P], w1_sc[:, 0:P], w1_bf[0][:, 0, :])
-        quantize(w1_codes[:, P : 2 * P], w1_sc[:, P : 2 * P], w1_bf[0][:, 1, :])
-        quantize(w1_codes[:, 2 * P :], w1_sc[:, 2 * P :], w1_bf[1][:].rearrange("p t c -> p (t c)"))
         h_sb = [tile(f"h_sb{t}", [P, S], F32) for t in range(PACK)]
-        pieces = [(0, 0, S // 2), (0, S // 2, S)] + [(t, 0, S) for t in range(1, PACK)]
-        for b, (t, j0, j1) in enumerate(pieces):
-            h_ps = ps.tile([P, j1 - j0], F32, name=f"h_ps{b}", tag=f"bank{b}")
+
+        def h_piece(b, t, codes, scales, j0, j1):
+            h_ps = bank(f"h_ps{b}", [P, j1 - j0], b)
             nc.tensor.matmul_mx(
-                out=h_ps[:], lhsT=w1_codes[:, t * P : (t + 1) * P].bitcast(FP8X4), lhsT_scale=w1_sc[:, t * P : (t + 1) * P],
+                out=h_ps[:], lhsT=codes.bitcast(FP8X4), lhsT_scale=scales,
                 rhs=x_codes[:, j0:j1].bitcast(FP8X4), rhs_scale=x_sc[:, j0:j1], start=True, stop=True,
             )
             nc.scalar.copy(out=h_sb[t][:, j0:j1], in_=h_ps[:])
 
-        e_codes = tile("e_codes", [P, V], U32, "w1bf0")
+        w1_bf = [tile(f"w1_bf{a}", [P, 2, P * PACK], BF16) for a in range(2)]
+        for c in range(2):
+            deal(nc.vector.tensor_copy, w1_bf[0][:], w1_raw[c], w1_cuts[c] // 32, 0)
+            deal(nc.scalar.copy, w1_bf[1][:], w1_raw[c], w1_cuts[c] // 32, 1)
+        w1_codes = tile("w1_codes", [P, H], U32)
+        w1_sc = tile("w1_sc", [P, H], U8)
+        quantize(w1_codes[:, 0:P], w1_sc[:, 0:P], w1_bf[0][:, 0, :])
+        quantize(w1_codes[:, P : 2 * P], w1_sc[:, P : 2 * P], w1_bf[0][:, 1, :])
+        quantize(w1_codes[:, 2 * P :], w1_sc[:, 2 * P :], w1_bf[1][:].rearrange("p t c -> p (t c)"))
+        pieces = [(0, 0, S // 2), (0, S // 2, S)] + [(t, 0, S) for t in range(1, PACK)]
+        for b, (t, j0, j1) in enumerate(pieces):
+            h_piece(b, t, w1_codes[:, t * P : (t + 1) * P], w1_sc[:, t * P : (t + 1) * P], j0, j1)
+
+        e_codes = tile("e_codes", [P, V], U32)
         e_sc = tile("e_sc", [P, V], U8)
-        nc.vector.tensor_copy(e_codes[:], ew_tab[:].bitcast(U32).indirect(usr_sb[:]))
         nc.vector.tensor_copy(e_sc[:], es_tab[:].indirect(usr_sb[:]))
+        nc.vector.tensor_copy(e_codes[:], ew_tab[:].bitcast(U32).indirect(usr_sb[:]))
 
-        both_terms = tile("both_terms", [P, 2, PACK, V], F32, "terms_w34codes")
-        terms = [both_terms[:, d] for d in range(2)]
-
-        w2_bf = tile("w2_bf", [P, PACK, P * PACK], BF16, "w2bf_term")
-        deal(nc.scalar.copy, w2_bf, w2_raw, 0, 0)
-        w34_bf = tile("w34_bf", [P, 2, N * PACK], BF16)
-        for s in range(2):
-            nc.scalar.copy(
-                out=w34_bf[:, s, :].rearrange("p (c i j) -> p c j i", i=4, j=PACK),
-                in_=w34_raw[:, s].rearrange("p j (c i) -> p c j i", i=4),
+        w2_bf = [tile(f"w2_bf{a}", [P, 2, P * PACK], BF16) for a in range(2)]
+        for c, a in ((0, 0), (0, 1), (1, 0)):
+            nc.gpsimd.tensor_copy(
+                out=w2_bf[a][:].rearrange("p e (b r j) -> p e b r j", r=8, j=PACK)[:, :, 8 * c : 8 * c + 8],
+                in_=w2_raw[c][:].rearrange("p j (b a r e) -> p a e b r j", a=2, r=8, e=2)[:, a],
             )
+        deal(nc.scalar.copy, w2_bf[1][:], w2_raw[1], 8, 1)
 
-        w2_codes = tile("w2_codes", [P, H], U32)
+        scaled = tile("scaled", [P, 2, 2, 2, P], F32)
+        for d in range(2):
+            turned = bank(f"turned{d}", [P, 2, 2, P], 5 + d)
+            for t in range(2):
+                picked = tile(f"picked{t}{d}", [P, V], F32)
+                nc.vector.tensor_copy(picked[:], h_sb[t][:].indirect(pos_sb[d][:]))
+                for u in range(2):
+                    nc.tensor.transpose(turned[:, u, t], picked[:, u * HALF : (u + 1) * HALF], ident[:])
+            for u in range(2):
+                nc.scalar.activation(
+                    out=scaled[:, d, u], in_=turned[:, u], func=COPY, scale=gate_col[:, 2 * d + u : 2 * d + u + 1]
+                )
+        z01_ps = bank("z01_ps", [P, 2, 2, HALF], 7)
+        for u in range(2):
+            for e in range(2):
+                for d in range(2):
+                    nc.tensor.matmul(
+                        z01_ps[:, u, e], lhsT=scaled[:, d, u, e], rhs=ident[:], is_transpose=True, start=(d == 0), stop=(d == 1)
+                    )
+
+        terms = tile("terms", [P, 2, 2, V], F32, "terms_w4bf")
+
+        def fused(e, d):
+            nc.vector.tensor_tensor(terms[:, d, e], h_sb[2 + e][:].indirect(pos_sb[d][:]), gate_sb[d][:], MULT)
+
+        fused(0, 0)
+        fused(1, 0)
+        fused(0, 1)
+        w2_codes = tile("w2_codes", [P, H], U32, "gate_sb0")
         w2_sc = tile("w2_sc", [P, H], U8)
-        for t in range(PACK):
-            for d in range(2):
-                nc.vector.tensor_tensor(terms[d][:, t, :], h_sb[t][:].indirect(pos_sb[d][:]), gate_sb[:, d, :], MULT)
-        quantize(w2_codes[:], w2_sc[:], w2_bf[:].rearrange("p t c -> p (t c)"))
-
-        gg_ps = [ps.tile([P, PACK, HALF], F32, name=f"gg_ps{u}") for u in range(2)]
+        for a in range(2):
+            cols = slice(2 * a * P, 2 * (a + 1) * P)
+            quantize(w2_codes[:, cols], w2_sc[:, cols], w2_bf[a][:].rearrange("p t c -> p (t c)"))
+        fused(1, 1)
+        gg_ps = [bank(f"gg_ps{u}", [P, PACK, HALF], 5 + u) for u in range(2)]
         for u in range(2):
             for t in range(PACK):
                 nc.tensor.matmul_mx(
@@ -150,29 +183,41 @@ def tile_picked_yngcf_none_p_kernel(
                     rhs_scale=e_sc[:, u * HALF : (u + 1) * HALF], start=True, stop=True,
                 )
 
-        z_all = tile("z_all", [P, 2, PACK, HALF], F32, "w2bf_term")
-        z = [z_all[:, u] for u in range(2)]
-        zy_bf = [tile(f"zy_bf{u}", [P, 2, HALF * PACK], BF16) for u in range(2)]
-        z_walk = [z[u].rearrange("p t (c i) -> p c t i", i=4) for u in range(2)]
+        w3_bf = tile("w3_bf", [P, N * PACK], BF16)
+        nc.scalar.copy(
+            out=w3_bf[:].rearrange("p (c i j) -> p c j i", i=4, j=PACK),
+            in_=w34_raw[0][:].rearrange("p j (c i) -> p c j i", i=4),
+        )
+        z_all = tile("z_all", [P, 2, PACK, HALF], F32, "w34_raw0")
+        nc.scalar.copy(out=z_all[:, :, 0:2], in_=z01_ps[:])
+        w34_codes = tile("w34_codes", [P, 2 * N], U32)
+        w34_sc = tile("w34_sc", [P, 2 * N], U8)
+        quantize(w34_codes[:, :N], w34_sc[:, :N], w3_bf[:])
         for u in range(2):
             users = slice(u * HALF, (u + 1) * HALF)
-            nc.vector.tensor_tensor(z[u], terms[0][:, :, users], terms[1][:, :, users], ADD)
-            nc.scalar.copy(out=zy_bf[u][:, 0, :].rearrange("p (c i t) -> p c t i", i=4, t=PACK), in_=z_walk[u])
-        w34_codes = tile("w34_codes", [P, 2 * N], U32, "terms_w34codes")
-        w34_sc = tile("w34_sc", [P, 2 * N], U8)
-        quantize(w34_codes[:], w34_sc[:], w34_bf[:].rearrange("p s c -> p (s c)"))
+            nc.vector.tensor_tensor(z_all[:, u, 2:4], terms[:, 0, :, users], terms[:, 1, :, users], ADD)
+        w4_bf = tile("w4_bf", [P, N * PACK], BF16, "terms_w4bf")
+        nc.gpsimd.tensor_scalar(
+            w4_bf[:].rearrange("p (c j) -> p c j", j=PACK), w34_raw[1][:].rearrange("p j c -> p c j"), 1.0, 0.0, MULT, ADD
+        )
+
+        z = [z_all[:, u] for u in range(2)]
+        zy_bf = [[tile(f"zy_bf{u}{s}", [P, HALF * PACK], BF16) for s in range(2)] for u in range(2)]
+        z_walk = [z[u].rearrange("p t (c i) -> p c t i", i=4) for u in range(2)]
         for u in range(2):
+            nc.scalar.copy(out=zy_bf[u][0][:].rearrange("p (c i t) -> p c t i", i=4, t=PACK), in_=z_walk[u])
             nc.vector.tensor_tensor(
-                zy_bf[u][:, 1, :].rearrange("p (c i t) -> p c t i", i=4, t=PACK),
+                zy_bf[u][1][:].rearrange("p (c i t) -> p c t i", i=4, t=PACK),
                 gg_ps[u][:].rearrange("p t (c i) -> p c t i", i=4), z_walk[u], MULT,
             )
+        quantize(w34_codes[:, N:], w34_sc[:, N:], w4_bf[:])
         for u in range(2):
             zy_codes = tile(f"zy_codes{u}", [P, 2 * HALF], U32)
             zy_sc = tile(f"zy_sc{u}", [P, 2 * HALF], U8)
-            out_ps = ps.tile([P, HALF], F32, name=f"out_ps{u}", tag=f"bank{u}")
+            out_ps = bank(f"out_ps{u}", [P, HALF], 2 + u)
             for s in range(2):
                 cols = slice(s * HALF, (s + 1) * HALF)
-                quantize(zy_codes[:, cols], zy_sc[:, cols], zy_bf[u][:, s, :])
+                quantize(zy_codes[:, cols], zy_sc[:, cols], zy_bf[u][s][:])
                 nc.tensor.matmul_mx(
                     out=out_ps[:], lhsT=w34_codes[:, s * N : (s + 1) * N].bitcast(FP8X4),
                     lhsT_scale=w34_sc[:, s * N : (s + 1) * N],

@@ -47,7 +47,7 @@ def tile_picked_yngcf_none_p_kernel(
         w34_raw = [tile(f"w34_raw{s}", [P, PACK, N], F32) for s in range(2)]
         xs_tab = tile("xs_tab", [P, T], U8)
         es_tab = tile("es_tab", [P, T], U8)
-        w1_cuts = (0, 5 * H // 8, H)
+        w1_cuts = (0, 3 * H // 4, H)
         w1_raw = [tile(f"w1_raw{c}", [P, PACK, w1_cuts[c + 1] - w1_cuts[c]], F32) for c in range(2)]
         ident = tile("ident", [P, P], F32)
 
@@ -74,9 +74,9 @@ def tile_picked_yngcf_none_p_kernel(
                 out=es_tab[32 * q : 32 * q + 4, :].bitcast(I32), in_=e_scales[0, 4 * q : 4 * q + 4, :].bitcast(I32)
             )
         load_words(ew_tab, e_words)
-        nc.sync.dma_start(out=w2_raw[0][:], in_=w2_rows[:, :, : H // 2])
         nc.sync.dma_start(pos_sb[0][:], pos1)
         nc.sync.dma_start(pos_sb[1][:], pos2)
+        nc.sync.dma_start(out=w2_raw[0][:], in_=w2_rows[:, :, : H // 2])
         nc.sync.dma_start(out=w2_raw[1][:], in_=w2_rows[:, :, H // 2 :])
         gate_rows = gate.rearrange("d p (u v) -> (d p u) v", u=2)
         with nc.allow_non_contiguous_dma(reason="one gate value a partition"):
@@ -132,12 +132,13 @@ def tile_picked_yngcf_none_p_kernel(
         nc.vector.tensor_copy(e_codes[:], ew_tab[:].bitcast(U32).indirect(usr_sb[:]))
 
         w2_bf = [tile(f"w2_bf{a}", [P, 2, P * PACK], BF16) for a in range(2)]
-        for c, a in ((0, 0), (0, 1), (1, 0)):
+        for c, a in ((0, 0), (0, 1)):
             nc.gpsimd.tensor_copy(
                 out=w2_bf[a][:].rearrange("p e (b r j) -> p e b r j", r=8, j=PACK)[:, :, 8 * c : 8 * c + 8],
                 in_=w2_raw[c][:].rearrange("p j (b a r e) -> p a e b r j", a=2, r=8, e=2)[:, a],
             )
-        deal(nc.scalar.copy, w2_bf[1][:], w2_raw[1], 8, 1)
+        for a in range(2):
+            deal(nc.scalar.copy, w2_bf[a][:], w2_raw[1], 8, a)
 
         scaled = tile("scaled", [P, 2, 2, 2, P], F32)
         for d in range(2):

@@ -74,30 +74,28 @@ def tile_picked_yngcf_none_p_kernel(
                 out=es_tab[32 * q : 32 * q + 4, :].bitcast(I32), in_=e_scales[0, 4 * q : 4 * q + 4, :].bitcast(I32)
             )
         load_words(ew_tab, e_words)
+        gate_rows = gate.rearrange("d p (u v) -> (d p u) v", u=2)
+        with nc.allow_non_contiguous_dma(reason="one gate value a partition"):
+            nc.sync.dma_start(out=gate_col[:], in_=gate_rows[0:388:129, :].rearrange("n v -> v n"))
         nc.sync.dma_start(pos_sb[0][:], pos1)
         nc.sync.dma_start(pos_sb[1][:], pos2)
         nc.sync.dma_start(out=w2_raw[0][:], in_=w2_rows[:, :, : H // 2])
         nc.sync.dma_start(out=w2_raw[1][:], in_=w2_rows[:, :, H // 2 :])
-        gate_rows = gate.rearrange("d p (u v) -> (d p u) v", u=2)
-        with nc.allow_non_contiguous_dma(reason="one gate value a partition"):
-            nc.sync.dma_start(out=gate_col[:], in_=gate_rows[0:388:129, :].rearrange("n v -> v n"))
         for d in range(2):
             nc.sync.dma_start(out=gate_sb[d][:], in_=gate[d])
         for s, w in enumerate((w3, w4)):
-            rows = w.rearrange("(b a x) c -> a b (x c)", a=2, x=16)
-            for a in range(2):
-                nc.sync.dma_start(out=w34_raw[s][:, 2 * a : 2 * a + 2].rearrange("p e c -> p (e c)"), in_=rows[a])
+            nc.sync.dma_start(out=w34_raw[s][:], in_=w.rearrange("(p j) c -> p j c", j=PACK))
 
         x_codes = tile("x_codes", [P, S], U32)
         x_sc = tile("x_sc", [P, S], U8)
         nc.vector.tensor_copy(x_sc[:], xs_tab[:].indirect(offs_sb[:]))
         nc.vector.tensor_copy(x_codes[:], xw_tab[:].bitcast(U32).indirect(offs_sb[:]))
 
-        def deal(copy, grouped, raw, b0, a):
-            n_b = raw.shape[2] // 32
+        def deal(copy, grouped, raw, m0, t0):
+            n_t, n_m = grouped.shape[1], raw.shape[2] // PACK
             copy(
-                out=grouped.rearrange("p e (b r j) -> p b r j e", r=8, j=PACK)[:, b0 : b0 + n_b],
-                in_=raw[:].rearrange("p j (b a r e) -> p a b r j e", a=2, r=8, e=2)[:, a],
+                out=grouped[:].rearrange("p t (m j) -> p m j t", j=PACK)[:, m0 : m0 + n_m],
+                in_=raw[:].rearrange("p j (m t) -> p m j t", t=PACK)[:, :, :, t0 : t0 + n_t],
             )
 
         def quantize(codes, scales, values):
@@ -115,8 +113,8 @@ def tile_picked_yngcf_none_p_kernel(
 
         w1_bf = [tile(f"w1_bf{a}", [P, 2, P * PACK], BF16) for a in range(2)]
         for c in range(2):
-            deal(nc.vector.tensor_copy, w1_bf[0][:], w1_raw[c], w1_cuts[c] // 32, 0)
-            deal(nc.scalar.copy, w1_bf[1][:], w1_raw[c], w1_cuts[c] // 32, 1)
+            deal(nc.vector.tensor_copy, w1_bf[0], w1_raw[c], w1_cuts[c] // PACK, 0)
+            deal(nc.scalar.copy, w1_bf[1], w1_raw[c], w1_cuts[c] // PACK, 2)
         w1_codes = tile("w1_codes", [P, H], U32)
         w1_sc = tile("w1_sc", [P, H], U8)
         quantize(w1_codes[:, 0:P], w1_sc[:, 0:P], w1_bf[0][:, 0, :])
@@ -131,16 +129,14 @@ def tile_picked_yngcf_none_p_kernel(
         nc.vector.tensor_copy(e_sc[:], es_tab[:].indirect(usr_sb[:]))
         nc.vector.tensor_copy(e_codes[:], ew_tab[:].bitcast(U32).indirect(usr_sb[:]))
 
-        w2_bf = [tile(f"w2_bf{a}", [P, 2, P * PACK], BF16) for a in range(2)]
-        for c, a in ((0, 0), (0, 1)):
-            nc.gpsimd.tensor_copy(
-                out=w2_bf[a][:].rearrange("p e (b r j) -> p e b r j", r=8, j=PACK)[:, :, 8 * c : 8 * c + 8],
-                in_=w2_raw[c][:].rearrange("p j (b a r e) -> p a e b r j", a=2, r=8, e=2)[:, a],
-            )
-        for a in range(2):
-            deal(nc.scalar.copy, w2_bf[a][:], w2_raw[1], 8, a)
+        w2_bf = tile("w2_bf", [P, PACK, P * PACK], BF16)
+        nc.gpsimd.tensor_scalar(
+            w2_bf[:].rearrange("p t (m j) -> p m t j", j=PACK)[:, : P // 2],
+            w2_raw[0][:].rearrange("p j (m t) -> p m t j", t=PACK), 1.0, 0.0, MULT, ADD,
+        )
+        deal(nc.scalar.copy, w2_bf, w2_raw[1], P // 2, 0)
 
-        scaled = tile("scaled", [P, 2, 2, 2, P], F32)
+        scaled = tile("scaled", [P, 2, 2, 2, P], F32, "w2_raw1")
         for d in range(2):
             turned = bank(f"turned{d}", [P, 2, 2, P], 5 + d)
             for t in range(2):
@@ -152,12 +148,12 @@ def tile_picked_yngcf_none_p_kernel(
                 nc.scalar.activation(
                     out=scaled[:, d, u], in_=turned[:, u], func=COPY, scale=gate_col[:, 2 * d + u : 2 * d + u + 1]
                 )
-        z01_ps = bank("z01_ps", [P, 2, 2, HALF], 7)
+        z01_ps = [bank(f"z01_ps{u}", [P, 2, HALF], (7, 0)[u]) for u in range(2)]
         for u in range(2):
             for e in range(2):
                 for d in range(2):
                     nc.tensor.matmul(
-                        z01_ps[:, u, e], lhsT=scaled[:, d, u, e], rhs=ident[:], is_transpose=True, start=(d == 0), stop=(d == 1)
+                        z01_ps[u][:, e], lhsT=scaled[:, d, u, e], rhs=ident[:], is_transpose=True, start=(d == 0), stop=(d == 1)
                     )
 
         terms = tile("terms", [P, 2, 2, V], F32, "terms_w4bf")
@@ -170,12 +166,12 @@ def tile_picked_yngcf_none_p_kernel(
         fused(0, 1)
         w2_codes = tile("w2_codes", [P, H], U32, "gate_sb0")
         w2_sc = tile("w2_sc", [P, H], U8)
-        for a in range(2):
-            cols = slice(2 * a * P, 2 * (a + 1) * P)
-            quantize(w2_codes[:, cols], w2_sc[:, cols], w2_bf[a][:].rearrange("p t c -> p (t c)"))
+        quantize(w2_codes[:], w2_sc[:], w2_bf[:].rearrange("p t c -> p (t c)"))
         fused(1, 1)
-        gg_ps = [bank(f"gg_ps{u}", [P, PACK, HALF], 5 + u) for u in range(2)]
-        for u in range(2):
+        gg_ps = []
+
+        def user_product(u):
+            gg_ps.append(bank(f"gg_ps{u}", [P, PACK, HALF], 6 + u))
             for t in range(PACK):
                 nc.tensor.matmul_mx(
                     out=gg_ps[u][:, t, :], lhsT=w2_codes[:, t * P : (t + 1) * P].bitcast(FP8X4),
@@ -184,13 +180,16 @@ def tile_picked_yngcf_none_p_kernel(
                     rhs_scale=e_sc[:, u * HALF : (u + 1) * HALF], start=True, stop=True,
                 )
 
+        user_product(0)
         w3_bf = tile("w3_bf", [P, N * PACK], BF16)
         nc.scalar.copy(
             out=w3_bf[:].rearrange("p (c i j) -> p c j i", i=4, j=PACK),
             in_=w34_raw[0][:].rearrange("p j (c i) -> p c j i", i=4),
         )
         z_all = tile("z_all", [P, 2, PACK, HALF], F32, "w34_raw0")
-        nc.scalar.copy(out=z_all[:, :, 0:2], in_=z01_ps[:])
+        for u in range(2):
+            nc.scalar.copy(out=z_all[:, u, 0:2], in_=z01_ps[u][:])
+        user_product(1)
         w34_codes = tile("w34_codes", [P, 2 * N], U32)
         w34_sc = tile("w34_sc", [P, 2 * N], U8)
         quantize(w34_codes[:, :N], w34_sc[:, :N], w3_bf[:])

@@ -43,7 +43,8 @@ def tile_picked_yngcf_none_p_kernel(
         ew_tab = tile("ew_tab", [P, T], I32)
         gate_col = tile("gate_col", [P, 4], F32)
         gate_sb = [tile(f"gate_sb{d}", [P, V], F32) for d in range(2)]
-        w2_raw = [tile(f"w2_raw{c}", [P, PACK, H // 2], F32) for c in range(2)]
+        w2_cuts = (0, H // 4, 3 * H // 4, H)
+        w2_raw = [tile(f"w2_raw{c}", [P, PACK, w2_cuts[c + 1] - w2_cuts[c]], F32) for c in range(3)]
         w34_raw = [tile(f"w34_raw{s}", [P, PACK, N], F32) for s in range(2)]
         xs_tab = tile("xs_tab", [P, T], U8)
         es_tab = tile("es_tab", [P, T], U8)
@@ -74,13 +75,14 @@ def tile_picked_yngcf_none_p_kernel(
                 out=es_tab[32 * q : 32 * q + 4, :].bitcast(I32), in_=e_scales[0, 4 * q : 4 * q + 4, :].bitcast(I32)
             )
         load_words(ew_tab, e_words)
+        nc.sync.dma_start(out=w2_raw[0][:], in_=w2_rows[:, :, : w2_cuts[1]])
+        nc.sync.dma_start(pos_sb[0][:], pos1)
+        nc.sync.dma_start(pos_sb[1][:], pos2)
+        for c in (1, 2):
+            nc.sync.dma_start(out=w2_raw[c][:], in_=w2_rows[:, :, w2_cuts[c] : w2_cuts[c + 1]])
         gate_rows = gate.rearrange("d p (u v) -> (d p u) v", u=2)
         with nc.allow_non_contiguous_dma(reason="one gate value a partition"):
             nc.sync.dma_start(out=gate_col[:], in_=gate_rows[0:388:129, :].rearrange("n v -> v n"))
-        nc.sync.dma_start(pos_sb[0][:], pos1)
-        nc.sync.dma_start(pos_sb[1][:], pos2)
-        nc.sync.dma_start(out=w2_raw[0][:], in_=w2_rows[:, :, : H // 2])
-        nc.sync.dma_start(out=w2_raw[1][:], in_=w2_rows[:, :, H // 2 :])
         for d in range(2):
             nc.sync.dma_start(out=gate_sb[d][:], in_=gate[d])
         for s, w in enumerate((w3, w4)):
@@ -130,13 +132,14 @@ def tile_picked_yngcf_none_p_kernel(
         nc.vector.tensor_copy(e_codes[:], ew_tab[:].bitcast(U32).indirect(usr_sb[:]))
 
         w2_bf = tile("w2_bf", [P, PACK, P * PACK], BF16)
-        nc.gpsimd.tensor_scalar(
-            w2_bf[:].rearrange("p t (m j) -> p m t j", j=PACK)[:, : P // 2],
-            w2_raw[0][:].rearrange("p j (m t) -> p m t j", t=PACK), 1.0, 0.0, MULT, ADD,
-        )
-        deal(nc.scalar.copy, w2_bf, w2_raw[1], P // 2, 0)
+        for c in range(2):
+            nc.gpsimd.tensor_scalar(
+                w2_bf[:].rearrange("p t (m j) -> p m t j", j=PACK)[:, w2_cuts[c] // PACK : w2_cuts[c + 1] // PACK],
+                w2_raw[c][:].rearrange("p j (m t) -> p m t j", t=PACK), 1.0, 0.0, MULT, ADD,
+            )
+        deal(nc.scalar.copy, w2_bf, w2_raw[2], w2_cuts[2] // PACK, 0)
 
-        scaled = tile("scaled", [P, 2, 2, 2, P], F32, "w2_raw1")
+        scaled = tile("scaled", [P, 2, 2, 2, P], F32, "w2_raw2")
         for d in range(2):
             turned = bank(f"turned{d}", [P, 2, 2, P], 5 + d)
             for t in range(2):
@@ -156,7 +159,7 @@ def tile_picked_yngcf_none_p_kernel(
                         z01_ps[u][:, e], lhsT=scaled[:, d, u, e], rhs=ident[:], is_transpose=True, start=(d == 0), stop=(d == 1)
                     )
 
-        terms = tile("terms", [P, 2, 2, V], F32, "terms_w4bf")
+        terms = tile("terms", [P, 2, 2, V], F32)
 
         def fused(e, d):
             nc.vector.tensor_tensor(terms[:, d, e], h_sb[2 + e][:].indirect(pos_sb[d][:]), gate_sb[d][:], MULT)
@@ -181,25 +184,22 @@ def tile_picked_yngcf_none_p_kernel(
                 )
 
         user_product(0)
-        w3_bf = tile("w3_bf", [P, N * PACK], BF16)
-        nc.scalar.copy(
-            out=w3_bf[:].rearrange("p (c i j) -> p c j i", i=4, j=PACK),
-            in_=w34_raw[0][:].rearrange("p j (c i) -> p c j i", i=4),
-        )
-        z_all = tile("z_all", [P, 2, PACK, HALF], F32, "w34_raw0")
+        w34_bf = tile("w34_bf", [P, 2, N * PACK], BF16)
+        for s in range(2):
+            nc.scalar.copy(
+                out=w34_bf[:, s].rearrange("p (c i j) -> p c j i", i=4, j=PACK),
+                in_=w34_raw[s][:].rearrange("p j (c i) -> p c j i", i=4),
+            )
+        z_all = tile("z_all", [P, 2, PACK, HALF], F32, "w34_raw1")
         for u in range(2):
             nc.scalar.copy(out=z_all[:, u, 0:2], in_=z01_ps[u][:])
         user_product(1)
         w34_codes = tile("w34_codes", [P, 2 * N], U32)
         w34_sc = tile("w34_sc", [P, 2 * N], U8)
-        quantize(w34_codes[:, :N], w34_sc[:, :N], w3_bf[:])
+        quantize(w34_codes[:], w34_sc[:], w34_bf[:].rearrange("p s c -> p (s c)"))
         for u in range(2):
             users = slice(u * HALF, (u + 1) * HALF)
             nc.vector.tensor_tensor(z_all[:, u, 2:4], terms[:, 0, :, users], terms[:, 1, :, users], ADD)
-        w4_bf = tile("w4_bf", [P, N * PACK], BF16, "terms_w4bf")
-        nc.gpsimd.tensor_scalar(
-            w4_bf[:].rearrange("p (c j) -> p c j", j=PACK), w34_raw[1][:].rearrange("p j c -> p c j"), 1.0, 0.0, MULT, ADD
-        )
 
         z = [z_all[:, u] for u in range(2)]
         zy_bf = [[tile(f"zy_bf{u}{s}", [P, HALF * PACK], BF16) for s in range(2)] for u in range(2)]
@@ -210,7 +210,6 @@ def tile_picked_yngcf_none_p_kernel(
                 zy_bf[u][1][:].rearrange("p (c i t) -> p c t i", i=4, t=PACK),
                 gg_ps[u][:].rearrange("p t (c i) -> p c t i", i=4), z_walk[u], MULT,
             )
-        quantize(w34_codes[:, N:], w34_sc[:, N:], w4_bf[:])
         for u in range(2):
             zy_codes = tile(f"zy_codes{u}", [P, 2 * HALF], U32)
             zy_sc = tile(f"zy_sc{u}", [P, 2 * HALF], U8)

@@ -28,10 +28,14 @@ def tile_picked_yngcf_none_p_kernel(
     nc = tc.nc
     with ExitStack() as ctx:
         sb = ctx.enter_context(tc.tile_pool(name="sb", bufs=1))
+        shared = ctx.enter_context(tc.tile_pool(name="shared", bufs=1))
         ps = ctx.enter_context(tc.psum_pool(name="ps", bufs=1))
 
         def tile(name, shape, dtype, tag=None):
             return sb.tile(shape, dtype, name=name, tag=tag or name, align_bytes=64)
+
+        def laid(name, shape, dtype, offset):
+            return shared.tile(shape, dtype, name=name, tag=name, align_bytes=64, offset=offset)
 
         def bank(name, shape, b):
             return ps.tile(shape, F32, name=name, tag=f"bank{b}")
@@ -42,14 +46,12 @@ def tile_picked_yngcf_none_p_kernel(
         xw_tab = tile("xw_tab", [P, T], I32)
         ew_tab = tile("ew_tab", [P, T], I32)
         gate_col = tile("gate_col", [P, 4], F32)
-        gate_sb = [tile(f"gate_sb{d}", [P, V], F32) for d in range(2)]
-        w2_cuts = (0, H // 4, 3 * H // 4, H)
-        w2_raw = [tile(f"w2_raw{c}", [P, PACK, w2_cuts[c + 1] - w2_cuts[c]], F32) for c in range(3)]
-        w34_raw = [tile(f"w34_raw{s}", [P, PACK, N], F32) for s in range(2)]
+        cuts = (0, 3 * H // 4, H)
+        w1_raw = [tile(f"w1_raw{c}", [P, PACK, cuts[c + 1] - cuts[c]], F32) for c in range(2)]
+        w2_raw = [tile("w2_raw0", [P, PACK, cuts[1]], F32), laid("w2_raw1", [P, PACK, H - cuts[1]], F32, 3072)]
+        w34_raw = laid("w34_raw", [P, 2, PACK, N], F32, 8192)
         xs_tab = tile("xs_tab", [P, T], U8)
         es_tab = tile("es_tab", [P, T], U8)
-        w1_cuts = (0, 3 * H // 4, H)
-        w1_raw = [tile(f"w1_raw{c}", [P, PACK, w1_cuts[c + 1] - w1_cuts[c]], F32) for c in range(2)]
         ident = tile("ident", [P, P], F32)
 
         def load_words(tab, words):
@@ -67,26 +69,23 @@ def tile_picked_yngcf_none_p_kernel(
                 in_=x_scales[0, 4 * q : 4 * q + 4, :].bitcast(I32).partition_broadcast(8),
             )
         load_words(xw_tab, x_words)
-        for c in range(2):
-            nc.sync.dma_start(out=w1_raw[c][:], in_=w1_rows[:, :, w1_cuts[c] : w1_cuts[c + 1]])
+        nc.sync.dma_start(out=w1_raw[0][:], in_=w1_rows[:, :, : cuts[1]])
         nc.sync.dma_start(usr_sb[:], usr)
+        nc.sync.dma_start(out=w1_raw[1][:], in_=w1_rows[:, :, cuts[1] :])
         for q in range(4):
             nc.sync.dma_start(
                 out=es_tab[32 * q : 32 * q + 4, :].bitcast(I32), in_=e_scales[0, 4 * q : 4 * q + 4, :].bitcast(I32)
             )
-        load_words(ew_tab, e_words)
-        nc.sync.dma_start(out=w2_raw[0][:], in_=w2_rows[:, :, : w2_cuts[1]])
+        nc.sync.dma_start(out=w2_raw[0][:], in_=w2_rows[:, :, : cuts[1]])
         nc.sync.dma_start(pos_sb[0][:], pos1)
         nc.sync.dma_start(pos_sb[1][:], pos2)
-        for c in (1, 2):
-            nc.sync.dma_start(out=w2_raw[c][:], in_=w2_rows[:, :, w2_cuts[c] : w2_cuts[c + 1]])
         gate_rows = gate.rearrange("d p (u v) -> (d p u) v", u=2)
         with nc.allow_non_contiguous_dma(reason="one gate value a partition"):
             nc.sync.dma_start(out=gate_col[:], in_=gate_rows[0:388:129, :].rearrange("n v -> v n"))
-        for d in range(2):
-            nc.sync.dma_start(out=gate_sb[d][:], in_=gate[d])
+        load_words(ew_tab, e_words)
+        nc.sync.dma_start(out=w2_raw[1][:], in_=w2_rows[:, :, cuts[1] :])
         for s, w in enumerate((w3, w4)):
-            nc.sync.dma_start(out=w34_raw[s][:], in_=w.rearrange("(p j) c -> p j c", j=PACK))
+            nc.sync.dma_start(out=w34_raw[:, s], in_=w.rearrange("(p j) c -> p j c", j=PACK))
 
         x_codes = tile("x_codes", [P, S], U32)
         x_sc = tile("x_sc", [P, S], U8)
@@ -115,8 +114,8 @@ def tile_picked_yngcf_none_p_kernel(
 
         w1_bf = [tile(f"w1_bf{a}", [P, 2, P * PACK], BF16) for a in range(2)]
         for c in range(2):
-            deal(nc.vector.tensor_copy, w1_bf[0], w1_raw[c], w1_cuts[c] // PACK, 0)
-            deal(nc.scalar.copy, w1_bf[1], w1_raw[c], w1_cuts[c] // PACK, 2)
+            deal(nc.vector.tensor_copy, w1_bf[0], w1_raw[c], cuts[c] // PACK, 0)
+            deal(nc.scalar.copy, w1_bf[1], w1_raw[c], cuts[c] // PACK, 2)
         w1_codes = tile("w1_codes", [P, H], U32)
         w1_sc = tile("w1_sc", [P, H], U8)
         quantize(w1_codes[:, 0:P], w1_sc[:, 0:P], w1_bf[0][:, 0, :])
@@ -129,52 +128,67 @@ def tile_picked_yngcf_none_p_kernel(
         e_codes = tile("e_codes", [P, V], U32)
         e_sc = tile("e_sc", [P, V], U8)
         nc.vector.tensor_copy(e_sc[:], es_tab[:].indirect(usr_sb[:]))
-        nc.vector.tensor_copy(e_codes[:], ew_tab[:].bitcast(U32).indirect(usr_sb[:]))
+
+
+        def pool_deal(grouped, raw):
+            nc.gpsimd.tensor_scalar(grouped, raw, 1.0, 0.0, MULT, ADD)
 
         w2_bf = tile("w2_bf", [P, PACK, P * PACK], BF16)
         for c in range(2):
-            nc.gpsimd.tensor_scalar(
-                w2_bf[:].rearrange("p t (m j) -> p m t j", j=PACK)[:, w2_cuts[c] // PACK : w2_cuts[c + 1] // PACK],
-                w2_raw[c][:].rearrange("p j (m t) -> p m t j", t=PACK), 1.0, 0.0, MULT, ADD,
+            pool_deal(
+                w2_bf[:].rearrange("p t (m j) -> p m t j", j=PACK)[:, cuts[c] // PACK : cuts[c + 1] // PACK],
+                w2_raw[c][:].rearrange("p j (m t) -> p m t j", t=PACK),
             )
-        deal(nc.scalar.copy, w2_bf, w2_raw[2], w2_cuts[2] // PACK, 0)
+        w34_bf = tile("w34_bf", [P, 2, N * PACK], BF16)
+        for s in range(2):
+            pool_deal(w34_bf[:, s].rearrange("p (c j) -> p c j", j=PACK), w34_raw[:, s].rearrange("p j c -> p c j"))
 
-        scaled = tile("scaled", [P, 2, 2, 2, P], F32, "w2_raw2")
-        for d in range(2):
-            turned = bank(f"turned{d}", [P, 2, 2, P], 5 + d)
-            for t in range(2):
-                picked = tile(f"picked{t}{d}", [P, V], F32)
-                nc.vector.tensor_copy(picked[:], h_sb[t][:].indirect(pos_sb[d][:]))
+        picked = [[tile(f"picked{t}{d}", [P, V], F32) for d in range(2)] for t in range(2)]
+        by_first = tile("by_first", [P, 2, V], F32)
+        by_second = [tile("by_second0", [P, V], F32), laid("by_second1", [P, V], F32, 4096)]
+        turned = [bank(f"turned{d}", [P, 2, 2, P], 5 + d) for d in range(2)]
+
+        def fetch(t, d):
+            dst = picked[t][d][:] if t < 2 else (by_first[:, t - 2], by_second[t - 2][:])[d]
+            src = h_sb[t][:].indirect(pos_sb[d][:])
+            if t == 0 or d == 1:
+                nc.vector.tensor_copy(dst, src)
+            else:
+                nc.scalar.activation(out=dst, in_=src, func=COPY)
+            if t < 2:
                 for u in range(2):
-                    nc.tensor.transpose(turned[:, u, t], picked[:, u * HALF : (u + 1) * HALF], ident[:])
+                    nc.tensor.transpose(turned[d][:, u, t], dst[:, u * HALF : (u + 1) * HALF], ident[:])
+
+        for t in range(PACK):
+            for d in range(2):
+                if (t, d) != (3, 1):
+                    fetch(t, d)
+
+        gates = bank("gates", [P, 2, V], 7)
+        for d in range(2):
             for u in range(2):
-                nc.scalar.activation(
-                    out=scaled[:, d, u], in_=turned[:, u], func=COPY, scale=gate_col[:, 2 * d + u : 2 * d + u + 1]
+                nc.tensor.transpose(
+                    gates[:, d, u * HALF : (u + 1) * HALF],
+                    gate_col[:, 2 * d + u : 2 * d + u + 1].to_broadcast([P, P]), ident[:],
                 )
-        z01_ps = [bank(f"z01_ps{u}", [P, 2, HALF], (7, 0)[u]) for u in range(2)]
-        for u in range(2):
-            for e in range(2):
-                for d in range(2):
-                    nc.tensor.matmul(
-                        z01_ps[u][:, e], lhsT=scaled[:, d, u, e], rhs=ident[:], is_transpose=True, start=(d == 0), stop=(d == 1)
-                    )
 
-        terms = tile("terms", [P, 2, 2, V], F32)
-
-        def fused(e, d):
-            nc.vector.tensor_tensor(terms[:, d, e], h_sb[2 + e][:].indirect(pos_sb[d][:]), gate_sb[d][:], MULT)
-
-        fused(0, 0)
-        fused(1, 0)
-        fused(0, 1)
-        w2_codes = tile("w2_codes", [P, H], U32, "gate_sb0")
+        nc.vector.tensor_copy(e_codes[:], ew_tab[:].bitcast(U32).indirect(usr_sb[:]))
+        w2_codes = tile("w2_codes", [P, H], U32)
         w2_sc = tile("w2_sc", [P, H], U8)
         quantize(w2_codes[:], w2_sc[:], w2_bf[:].rearrange("p t c -> p (t c)"))
-        fused(1, 1)
-        gg_ps = []
+        fetch(3, 1)
 
-        def user_product(u):
-            gg_ps.append(bank(f"gg_ps{u}", [P, PACK, HALF], 6 + u))
+        scaled = laid("scaled", [P, 2, 2, 2, P], F32, 0)
+        terms = tile("terms", [P, 2, 2, V], F32, "w2_bf")
+        z = [laid(f"z{u}", [P, PACK, HALF], F32, 8192 + 2048 * u) for u in range(2)]
+        gg_ps, z01_ps = [], []
+        for u in range(2):
+            for d in (1, 0):
+                nc.scalar.activation(
+                    out=scaled[:, d, u], in_=turned[d][:, u], func=COPY, scale=gate_col[:, 2 * d + u : 2 * d + u + 1]
+                )
+        for u in range(2):
+            gg_ps.append(bank(f"gg_ps{u}", [P, PACK, HALF], 2 + u))
             for t in range(PACK):
                 nc.tensor.matmul_mx(
                     out=gg_ps[u][:, t, :], lhsT=w2_codes[:, t * P : (t + 1) * P].bitcast(FP8X4),
@@ -182,38 +196,39 @@ def tile_picked_yngcf_none_p_kernel(
                     rhs=e_codes[:, u * HALF : (u + 1) * HALF].bitcast(FP8X4),
                     rhs_scale=e_sc[:, u * HALF : (u + 1) * HALF], start=True, stop=True,
                 )
-
-        user_product(0)
-        w34_bf = tile("w34_bf", [P, 2, N * PACK], BF16)
-        for s in range(2):
-            nc.scalar.copy(
-                out=w34_bf[:, s].rearrange("p (c i j) -> p c j i", i=4, j=PACK),
-                in_=w34_raw[s][:].rearrange("p j (c i) -> p c j i", i=4),
-            )
-        z_all = tile("z_all", [P, 2, PACK, HALF], F32, "w34_raw1")
         for u in range(2):
-            nc.scalar.copy(out=z_all[:, u, 0:2], in_=z01_ps[u][:])
-        user_product(1)
+            z01_ps.append(bank(f"z01_ps{u}", [P, 2, HALF], u))
+            for e in range(2):
+                for d in range(2):
+                    nc.tensor.matmul(
+                        z01_ps[u][:, e], lhsT=scaled[:, d, u, e], rhs=ident[:], is_transpose=True, start=(d == 0), stop=(d == 1)
+                    )
+        nc.vector.tensor_tensor(terms[:, 0], by_first[:], gates[:, 0].unsqueeze(1).to_broadcast([P, 2, V]), MULT)
+        for e in (1, 0):
+            nc.vector.tensor_tensor(terms[:, 1, e], by_second[e][:], gates[:, 1], MULT)
         w34_codes = tile("w34_codes", [P, 2 * N], U32)
         w34_sc = tile("w34_sc", [P, 2 * N], U8)
         quantize(w34_codes[:], w34_sc[:], w34_bf[:].rearrange("p s c -> p (s c)"))
         for u in range(2):
             users = slice(u * HALF, (u + 1) * HALF)
-            nc.vector.tensor_tensor(z_all[:, u, 2:4], terms[:, 0, :, users], terms[:, 1, :, users], ADD)
+            nc.vector.tensor_tensor(z[u][:, 2:4], terms[:, 0, :, users], terms[:, 1, :, users], ADD)
+            nc.scalar.copy(out=z[u][:, 0:2], in_=z01_ps[u][:])
 
-        z = [z_all[:, u] for u in range(2)]
         zy_bf = [[tile(f"zy_bf{u}{s}", [P, HALF * PACK], BF16) for s in range(2)] for u in range(2)]
-        z_walk = [z[u].rearrange("p t (c i) -> p c t i", i=4) for u in range(2)]
         for u in range(2):
-            nc.scalar.copy(out=zy_bf[u][0][:].rearrange("p (c i t) -> p c t i", i=4, t=PACK), in_=z_walk[u])
+            z_walk = z[u][:].rearrange("p t (c i) -> p c t i", i=4)
+            if u == 0:
+                pool_deal(zy_bf[u][0][:].rearrange("p (c t) -> p c t", t=PACK), z[u][:].rearrange("p t c -> p c t"))
+            else:
+                nc.scalar.copy(out=zy_bf[u][0][:].rearrange("p (c i t) -> p c t i", i=4, t=PACK), in_=z_walk)
             nc.vector.tensor_tensor(
                 zy_bf[u][1][:].rearrange("p (c i t) -> p c t i", i=4, t=PACK),
-                gg_ps[u][:].rearrange("p t (c i) -> p c t i", i=4), z_walk[u], MULT,
+                gg_ps[u][:].rearrange("p t (c i) -> p c t i", i=4), z_walk, MULT,
             )
         for u in range(2):
             zy_codes = tile(f"zy_codes{u}", [P, 2 * HALF], U32)
             zy_sc = tile(f"zy_sc{u}", [P, 2 * HALF], U8)
-            out_ps = bank(f"out_ps{u}", [P, HALF], 2 + u)
+            out_ps = bank(f"out_ps{u}", [P, HALF], 4 + u)
             for s in range(2):
                 cols = slice(s * HALF, (s + 1) * HALF)
                 quantize(zy_codes[:, cols], zy_sc[:, cols], zy_bf[u][s][:])

@@ -49,7 +49,7 @@ def tile_picked_yngcf_none_p_kernel(
         cuts = (0, 3 * H // 4, H)
         w1_raw = [tile(f"w1_raw{c}", [P, PACK, cuts[c + 1] - cuts[c]], F32) for c in range(2)]
         w2_raw = [tile("w2_raw0", [P, PACK, cuts[1]], F32), laid("w2_raw1", [P, PACK, H - cuts[1]], F32, 3072)]
-        w34_raw = laid("w34_raw", [P, 2, PACK, N], F32, 8192)
+        w34_raw = [tile(f"w34_raw{s}", [P, PACK, N], F32) for s in range(2)]
         xs_tab = tile("xs_tab", [P, T], U8)
         es_tab = tile("es_tab", [P, T], U8)
         ident = tile("ident", [P, P], F32)
@@ -85,7 +85,7 @@ def tile_picked_yngcf_none_p_kernel(
         load_words(ew_tab, e_words)
         nc.sync.dma_start(out=w2_raw[1][:], in_=w2_rows[:, :, cuts[1] :])
         for s, w in enumerate((w3, w4)):
-            nc.sync.dma_start(out=w34_raw[:, s], in_=w.rearrange("(p j) c -> p j c", j=PACK))
+            nc.sync.dma_start(out=w34_raw[s][:], in_=w.rearrange("(p j) c -> p j c", j=PACK))
 
         x_codes = tile("x_codes", [P, S], U32)
         x_sc = tile("x_sc", [P, S], U8)
@@ -133,15 +133,12 @@ def tile_picked_yngcf_none_p_kernel(
         def pool_deal(grouped, raw):
             nc.gpsimd.tensor_scalar(grouped, raw, 1.0, 0.0, MULT, ADD)
 
-        w2_bf = tile("w2_bf", [P, PACK, P * PACK], BF16)
+        w2_bf = laid("w2_bf", [P, PACK, P * PACK], BF16, 8192 + 1024)
         for c in range(2):
             pool_deal(
                 w2_bf[:].rearrange("p t (m j) -> p m t j", j=PACK)[:, cuts[c] // PACK : cuts[c + 1] // PACK],
                 w2_raw[c][:].rearrange("p j (m t) -> p m t j", t=PACK),
             )
-        w34_bf = tile("w34_bf", [P, 2, N * PACK], BF16)
-        for s in range(2):
-            pool_deal(w34_bf[:, s].rearrange("p (c j) -> p c j", j=PACK), w34_raw[:, s].rearrange("p j c -> p c j"))
 
         picked = [[tile(f"picked{t}{d}", [P, V], F32) for d in range(2)] for t in range(2)]
         by_first = tile("by_first", [P, 2, V], F32)
@@ -177,16 +174,22 @@ def tile_picked_yngcf_none_p_kernel(
         w2_sc = tile("w2_sc", [P, H], U8)
         quantize(w2_codes[:], w2_sc[:], w2_bf[:].rearrange("p t c -> p (t c)"))
         fetch(3, 1)
+        w34_bf = [laid("w3_bf", [P, N * PACK], BF16, 8192 + 4096), tile("w4_bf", [P, N * PACK], BF16)]
+        pool_deal(w34_bf[0][:].rearrange("p (c j) -> p c j", j=PACK), w34_raw[0][:].rearrange("p j c -> p c j"))
 
         scaled = laid("scaled", [P, 2, 2, 2, P], F32, 0)
-        terms = tile("terms", [P, 2, 2, V], F32, "w2_bf")
-        z = [laid(f"z{u}", [P, PACK, HALF], F32, 8192 + 2048 * u) for u in range(2)]
+        terms = laid("terms", [P, 2, 2, V], F32, 8192)
+        z = [tile(f"z{u}", [P, PACK, HALF], F32) for u in range(2)]
         gg_ps, z01_ps = [], []
         for u in range(2):
             for d in (1, 0):
                 nc.scalar.activation(
                     out=scaled[:, d, u], in_=turned[d][:, u], func=COPY, scale=gate_col[:, 2 * d + u : 2 * d + u + 1]
                 )
+        nc.scalar.copy(
+            out=w34_bf[1][:].rearrange("p (c i j) -> p c j i", i=4, j=PACK),
+            in_=w34_raw[1][:].rearrange("p j (c i) -> p c j i", i=4),
+        )
         for u in range(2):
             gg_ps.append(bank(f"gg_ps{u}", [P, PACK, HALF], 2 + u))
             for t in range(PACK):
@@ -208,11 +211,12 @@ def tile_picked_yngcf_none_p_kernel(
             nc.vector.tensor_tensor(terms[:, 1, e], by_second[e][:], gates[:, 1], MULT)
         w34_codes = tile("w34_codes", [P, 2 * N], U32)
         w34_sc = tile("w34_sc", [P, 2 * N], U8)
-        quantize(w34_codes[:], w34_sc[:], w34_bf[:].rearrange("p s c -> p (s c)"))
+        quantize(w34_codes[:, :N], w34_sc[:, :N], w34_bf[0][:])
         for u in range(2):
             users = slice(u * HALF, (u + 1) * HALF)
             nc.vector.tensor_tensor(z[u][:, 2:4], terms[:, 0, :, users], terms[:, 1, :, users], ADD)
             nc.scalar.copy(out=z[u][:, 0:2], in_=z01_ps[u][:])
+        quantize(w34_codes[:, N:], w34_sc[:, N:], w34_bf[1][:])
 
         zy_bf = [[tile(f"zy_bf{u}{s}", [P, HALF * PACK], BF16) for s in range(2)] for u in range(2)]
         for u in range(2):

@@ -142,7 +142,7 @@ def tile_picked_yngcf_none_p_kernel(
 
         picked = [[tile(f"picked{t}{d}", [P, V], F32) for d in range(2)] for t in range(2)]
         by_first = tile("by_first", [P, 2, V], F32)
-        by_second = [tile("by_second0", [P, V], F32), laid("by_second1", [P, V], F32, 4096)]
+        by_second = [tile("by_second0", [P, V], F32), laid("by_second1", [P, V], F32, 3136)]
         turned = [bank(f"turned{d}", [P, 2, 2, P], 5 + d) for d in range(2)]
 
         def fetch(t, d):
@@ -174,24 +174,21 @@ def tile_picked_yngcf_none_p_kernel(
         w2_sc = tile("w2_sc", [P, H], U8)
         quantize(w2_codes[:], w2_sc[:], w2_bf[:].rearrange("p t c -> p (t c)"))
         fetch(3, 1)
-        w34_bf = [laid("w3_bf", [P, N * PACK], BF16, 8192 + 4096), tile("w4_bf", [P, N * PACK], BF16)]
+        w34_bf = [laid("w3_bf", [P, N * PACK], BF16, 8192 + 4096), laid("w4_bf", [P, N * PACK], BF16, 1088)]
         pool_deal(w34_bf[0][:].rearrange("p (c j) -> p c j", j=PACK), w34_raw[0][:].rearrange("p j c -> p c j"))
 
-        scaled = laid("scaled", [P, 2, 2, 2, P], F32, 0)
+        scaled = [laid(f"scaled{u}", [P, 2, 2, P], F32, (1088, 4160)[u]) for u in range(2)]
         terms = laid("terms", [P, 2, 2, V], F32, 8192)
         z = [tile(f"z{u}", [P, PACK, HALF], F32) for u in range(2)]
         gg_ps, z01_ps = [], []
         for u in range(2):
             for d in (1, 0):
                 nc.scalar.activation(
-                    out=scaled[:, d, u], in_=turned[d][:, u], func=COPY, scale=gate_col[:, 2 * d + u : 2 * d + u + 1]
+                    out=scaled[u][:, d], in_=turned[d][:, u], func=COPY, scale=gate_col[:, 2 * d + u : 2 * d + u + 1]
                 )
-        nc.scalar.copy(
-            out=w34_bf[1][:].rearrange("p (c i j) -> p c j i", i=4, j=PACK),
-            in_=w34_raw[1][:].rearrange("p j (c i) -> p c j i", i=4),
-        )
-        for u in range(2):
-            gg_ps.append(bank(f"gg_ps{u}", [P, PACK, HALF], 2 + u))
+
+        def user_product(u):
+            gg_ps.append(bank(f"gg_ps{u}", [P, PACK, HALF], (2, 5)[u]))
             for t in range(PACK):
                 nc.tensor.matmul_mx(
                     out=gg_ps[u][:, t, :], lhsT=w2_codes[:, t * P : (t + 1) * P].bitcast(FP8X4),
@@ -199,26 +196,38 @@ def tile_picked_yngcf_none_p_kernel(
                     rhs=e_codes[:, u * HALF : (u + 1) * HALF].bitcast(FP8X4),
                     rhs_scale=e_sc[:, u * HALF : (u + 1) * HALF], start=True, stop=True,
                 )
+
+        user_product(0)
         for u in range(2):
             z01_ps.append(bank(f"z01_ps{u}", [P, 2, HALF], u))
             for e in range(2):
                 for d in range(2):
                     nc.tensor.matmul(
-                        z01_ps[u][:, e], lhsT=scaled[:, d, u, e], rhs=ident[:], is_transpose=True, start=(d == 0), stop=(d == 1)
+                        z01_ps[u][:, e], lhsT=scaled[u][:, d, e], rhs=ident[:], is_transpose=True, start=(d == 0), stop=(d == 1)
                     )
+        user_product(1)
         nc.vector.tensor_tensor(terms[:, 0], by_first[:], gates[:, 0].unsqueeze(1).to_broadcast([P, 2, V]), MULT)
-        for e in (1, 0):
-            nc.vector.tensor_tensor(terms[:, 1, e], by_second[e][:], gates[:, 1], MULT)
-        w34_codes = tile("w34_codes", [P, 2 * N], U32)
+        nc.vector.tensor_tensor(terms[:, 1, 0], by_second[0][:], gates[:, 1], MULT)
+        for u in range(2):
+            users = slice(u * HALF, (u + 1) * HALF)
+            nc.vector.tensor_tensor(terms[:, 1, 1, users], by_second[1][:, users], gates[:, 1, users], MULT)
         w34_sc = tile("w34_sc", [P, 2 * N], U8)
-        quantize(w34_codes[:, :N], w34_sc[:, :N], w34_bf[0][:])
+        w34_codes = [tile("w3_codes", [P, N], U32)]
+        quantize(w34_codes[0][:], w34_sc[:, :N], w34_bf[0][:])
         for u in range(2):
             users = slice(u * HALF, (u + 1) * HALF)
             nc.vector.tensor_tensor(z[u][:, 2:4], terms[:, 0, :, users], terms[:, 1, :, users], ADD)
             nc.scalar.copy(out=z[u][:, 0:2], in_=z01_ps[u][:])
-        quantize(w34_codes[:, N:], w34_sc[:, N:], w34_bf[1][:])
+            if u == 0:
+                nc.scalar.copy(
+                    out=w34_bf[1][:].rearrange("p (c i j) -> p c j i", i=4, j=PACK),
+                    in_=w34_raw[1][:].rearrange("p j (c i) -> p c j i", i=4),
+                )
 
-        zy_bf = [[tile(f"zy_bf{u}{s}", [P, HALF * PACK], BF16) for s in range(2)] for u in range(2)]
+        zy_bf = [
+            [laid("z0_bf", [P, HALF * PACK], BF16, 8192), tile("y0_bf", [P, HALF * PACK], BF16)],
+            [tile("z1_bf", [P, HALF * PACK], BF16), tile("y1_bf", [P, HALF * PACK], BF16)],
+        ]
         for u in range(2):
             z_walk = z[u][:].rearrange("p t (c i) -> p c t i", i=4)
             if u == 0:
@@ -229,15 +238,17 @@ def tile_picked_yngcf_none_p_kernel(
                 zy_bf[u][1][:].rearrange("p (c i t) -> p c t i", i=4, t=PACK),
                 gg_ps[u][:].rearrange("p t (c i) -> p c t i", i=4), z_walk, MULT,
             )
+        w34_codes.append(tile("w4_codes", [P, N], U32, "z0"))
+        quantize(w34_codes[1][:], w34_sc[:, N:], w34_bf[1][:])
         for u in range(2):
             zy_codes = tile(f"zy_codes{u}", [P, 2 * HALF], U32)
             zy_sc = tile(f"zy_sc{u}", [P, 2 * HALF], U8)
-            out_ps = bank(f"out_ps{u}", [P, HALF], 4 + u)
+            out_ps = bank(f"out_ps{u}", [P, HALF], 3 + u)
             for s in range(2):
                 cols = slice(s * HALF, (s + 1) * HALF)
                 quantize(zy_codes[:, cols], zy_sc[:, cols], zy_bf[u][s][:])
                 nc.tensor.matmul_mx(
-                    out=out_ps[:], lhsT=w34_codes[:, s * N : (s + 1) * N].bitcast(FP8X4),
+                    out=out_ps[:], lhsT=w34_codes[s][:].bitcast(FP8X4),
                     lhsT_scale=w34_sc[:, s * N : (s + 1) * N],
                     rhs=zy_codes[:, cols].bitcast(FP8X4), rhs_scale=zy_sc[:, cols], start=(s == 0), stop=(s == 1),
                 )

@@ -200,17 +200,20 @@ def tile_picked_yngcf_none_p_kernel(
         user_product(0)
         for u in range(2):
             z01_ps.append(bank(f"z01_ps{u}", [P, 2, HALF], u))
-            for e in range(2):
-                for d in range(2):
-                    nc.tensor.matmul(
-                        z01_ps[u][:, e], lhsT=scaled[u][:, d, e], rhs=ident[:], is_transpose=True, start=(d == 0), stop=(d == 1)
-                    )
+            passes = [(d, e) for d in (1, 0) for e in range(2)] if u else [(d, e) for e in range(2) for d in range(2)]
+            for d, e in passes:
+                nc.tensor.matmul(
+                    z01_ps[u][:, e], lhsT=scaled[u][:, d, e], rhs=ident[:], is_transpose=True,
+                    start=(d, e) == (1, 0) if u else d == 0, stop=(d, e) == (0, 1) if u else d == 1,
+                )
         user_product(1)
-        nc.vector.tensor_tensor(terms[:, 0], by_first[:], gates[:, 0].unsqueeze(1).to_broadcast([P, 2, V]), MULT)
-        nc.vector.tensor_tensor(terms[:, 1, 0], by_second[0][:], gates[:, 1], MULT)
+        for e in range(2):
+            nc.vector.tensor_tensor(terms[:, 1, e], by_second[e][:], gates[:, 1], MULT)
         for u in range(2):
             users = slice(u * HALF, (u + 1) * HALF)
-            nc.vector.tensor_tensor(terms[:, 1, 1, users], by_second[1][:, users], gates[:, 1, users], MULT)
+            nc.vector.tensor_tensor(
+                terms[:, 0, :, users], by_first[:, :, users], gates[:, 0, users].unsqueeze(1).to_broadcast([P, 2, HALF]), MULT
+            )
         w34_sc = tile("w34_sc", [P, 2 * N], U8)
         w34_codes = [tile("w3_codes", [P, N], U32)]
         quantize(w34_codes[0][:], w34_sc[:, :N], w34_bf[0][:])

@@ -142,24 +142,26 @@ def tile_picked_yngcf_none_p_kernel(
 
         picked = [[tile(f"picked{t}{d}", [P, V], F32) for d in range(2)] for t in range(2)]
         by_first = tile("by_first", [P, 2, V], F32)
-        by_second = [tile("by_second0", [P, V], F32), laid("by_second1", [P, V], F32, 3136)]
+        by_second = tile("by_second", [P, V], F32)
+        last = [laid("last0", [P, HALF], F32, 3136), tile("last1", [P, HALF], F32)]
         turned = [bank(f"turned{d}", [P, 2, 2, P], 5 + d) for d in range(2)]
 
-        def fetch(t, d):
-            dst = picked[t][d][:] if t < 2 else (by_first[:, t - 2], by_second[t - 2][:])[d]
-            src = h_sb[t][:].indirect(pos_sb[d][:])
-            if t == 0 or d == 1:
+        def fetch(on_vector, dst, t, offsets):
+            src = h_sb[t][:].indirect(offsets)
+            if on_vector:
                 nc.vector.tensor_copy(dst, src)
             else:
                 nc.scalar.activation(out=dst, in_=src, func=COPY)
-            if t < 2:
-                for u in range(2):
-                    nc.tensor.transpose(turned[d][:, u, t], dst[:, u * HALF : (u + 1) * HALF], ident[:])
 
-        for t in range(PACK):
+        for t in range(2):
             for d in range(2):
-                if (t, d) != (3, 1):
-                    fetch(t, d)
+                fetch(t == 0 or d == 1, picked[t][d][:], t, pos_sb[d][:])
+                for u in range(2):
+                    nc.tensor.transpose(turned[d][:, u, t], picked[t][d][:, u * HALF : (u + 1) * HALF], ident[:])
+        for e in range(2):
+            fetch(False, by_first[:, e], 2 + e, pos_sb[0][:])
+        fetch(True, by_second[:], 2, pos_sb[1][:])
+        fetch(False, last[1][:], 3, pos_sb[1][:, HALF // 16 :])
 
         gates = bank("gates", [P, 2, V], 7)
         for d in range(2):
@@ -173,9 +175,12 @@ def tile_picked_yngcf_none_p_kernel(
         w2_codes = tile("w2_codes", [P, H], U32)
         w2_sc = tile("w2_sc", [P, H], U8)
         quantize(w2_codes[:], w2_sc[:], w2_bf[:].rearrange("p t c -> p (t c)"))
-        fetch(3, 1)
-        w34_bf = [laid("w3_bf", [P, N * PACK], BF16, 8192 + 4096), laid("w4_bf", [P, N * PACK], BF16, 1088)]
-        pool_deal(w34_bf[0][:].rearrange("p (c j) -> p c j", j=PACK), w34_raw[0][:].rearrange("p j c -> p c j"))
+        fetch(True, last[0][:], 3, pos_sb[1][:, : HALF // 16])
+        w34_bf = laid("w34_bf", [P, 2, N * PACK], BF16, 8192 + 4096)
+        pool_deal(w34_bf[:, 0].rearrange("p (c j) -> p c j", j=PACK), w34_raw[0][:].rearrange("p j c -> p c j"))
+        pool_deal(
+            w34_bf[:, 1].rearrange("p (c j) -> p c j", j=PACK)[:, : N // 4], w34_raw[1][:].rearrange("p j c -> p c j")[:, : N // 4]
+        )
 
         scaled = [laid(f"scaled{u}", [P, 2, 2, P], F32, (1088, 4160)[u]) for u in range(2)]
         terms = laid("terms", [P, 2, 2, V], F32, 8192)
@@ -207,24 +212,22 @@ def tile_picked_yngcf_none_p_kernel(
                     start=(d, e) == (1, 0) if u else d == 0, stop=(d, e) == (0, 1) if u else d == 1,
                 )
         user_product(1)
-        for e in range(2):
-            nc.vector.tensor_tensor(terms[:, 1, e], by_second[e][:], gates[:, 1], MULT)
+        nc.vector.tensor_tensor(terms[:, 1, 0], by_second[:], gates[:, 1], MULT)
+        nc.vector.tensor_tensor(terms[:, 1, 1, :HALF], last[0][:], gates[:, 1, :HALF], MULT)
         for u in range(2):
             users = slice(u * HALF, (u + 1) * HALF)
             nc.vector.tensor_tensor(
                 terms[:, 0, :, users], by_first[:, :, users], gates[:, 0, users].unsqueeze(1).to_broadcast([P, 2, HALF]), MULT
             )
-        w34_sc = tile("w34_sc", [P, 2 * N], U8)
-        w34_codes = [tile("w3_codes", [P, N], U32)]
-        quantize(w34_codes[0][:], w34_sc[:, :N], w34_bf[0][:])
+        nc.vector.tensor_tensor(terms[:, 1, 1, HALF:], last[1][:], gates[:, 1, HALF:], MULT)
         for u in range(2):
             users = slice(u * HALF, (u + 1) * HALF)
             nc.vector.tensor_tensor(z[u][:, 2:4], terms[:, 0, :, users], terms[:, 1, :, users], ADD)
             nc.scalar.copy(out=z[u][:, 0:2], in_=z01_ps[u][:])
             if u == 0:
                 nc.scalar.copy(
-                    out=w34_bf[1][:].rearrange("p (c i j) -> p c j i", i=4, j=PACK),
-                    in_=w34_raw[1][:].rearrange("p j (c i) -> p c j i", i=4),
+                    out=w34_bf[:, 1].rearrange("p (c i j) -> p c j i", i=4, j=PACK)[:, N // 16 :],
+                    in_=w34_raw[1][:].rearrange("p j (c i) -> p c j i", i=4)[:, N // 16 :],
                 )
 
         zy_bf = [
@@ -241,8 +244,9 @@ def tile_picked_yngcf_none_p_kernel(
                 zy_bf[u][1][:].rearrange("p (c i t) -> p c t i", i=4, t=PACK),
                 gg_ps[u][:].rearrange("p t (c i) -> p c t i", i=4), z_walk, MULT,
             )
-        w34_codes.append(tile("w4_codes", [P, N], U32, "z0"))
-        quantize(w34_codes[1][:], w34_sc[:, N:], w34_bf[1][:])
+        w34_codes = tile("w34_codes", [P, 2 * N], U32, "z0")
+        w34_sc = tile("w34_sc", [P, 2 * N], U8)
+        quantize(w34_codes[:], w34_sc[:], w34_bf[:].rearrange("p s c -> p (s c)"))
         for u in range(2):
             zy_codes = tile(f"zy_codes{u}", [P, 2 * HALF], U32)
             zy_sc = tile(f"zy_sc{u}", [P, 2 * HALF], U8)
@@ -251,7 +255,7 @@ def tile_picked_yngcf_none_p_kernel(
                 cols = slice(s * HALF, (s + 1) * HALF)
                 quantize(zy_codes[:, cols], zy_sc[:, cols], zy_bf[u][s][:])
                 nc.tensor.matmul_mx(
-                    out=out_ps[:], lhsT=w34_codes[s][:].bitcast(FP8X4),
+                    out=out_ps[:], lhsT=w34_codes[:, s * N : (s + 1) * N].bitcast(FP8X4),
                     lhsT_scale=w34_sc[:, s * N : (s + 1) * N],
                     rhs=zy_codes[:, cols].bitcast(FP8X4), rhs_scale=zy_sc[:, cols], start=(s == 0), stop=(s == 1),
                 )

@@ -47,7 +47,7 @@ def tile_picked_yngcf_none_p_kernel(
         ew_tab = tile("ew_tab", [P, T], I32)
         gate_col = tile("gate_col", [P, 4], F32)
         cuts = (0, 3 * H // 4, H)
-        w1_raw = [tile(f"w1_raw{c}", [P, PACK, cuts[c + 1] - cuts[c]], F32) for c in range(2)]
+        w1_raw = [tile(f"w1_raw{c}", [P, PACK, H // 2], F32) for c in range(2)]
         w2_raw = [tile("w2_raw0", [P, PACK, cuts[1]], F32), laid("w2_raw1", [P, PACK, H - cuts[1]], F32, 3072)]
         w34_raw = [tile(f"w34_raw{s}", [P, PACK, N], F32) for s in range(2)]
         xs_tab = tile("xs_tab", [P, T], U8)
@@ -69,9 +69,9 @@ def tile_picked_yngcf_none_p_kernel(
                 in_=x_scales[0, 4 * q : 4 * q + 4, :].bitcast(I32).partition_broadcast(8),
             )
         load_words(xw_tab, x_words)
-        nc.sync.dma_start(out=w1_raw[0][:], in_=w1_rows[:, :, : cuts[1]])
+        nc.sync.dma_start(out=w1_raw[0][:], in_=w1_rows[:, :, : H // 2])
         nc.sync.dma_start(usr_sb[:], usr)
-        nc.sync.dma_start(out=w1_raw[1][:], in_=w1_rows[:, :, cuts[1] :])
+        nc.sync.dma_start(out=w1_raw[1][:], in_=w1_rows[:, :, H // 2 :])
         for q in range(4):
             nc.sync.dma_start(
                 out=es_tab[32 * q : 32 * q + 4, :].bitcast(I32), in_=e_scales[0, 4 * q : 4 * q + 4, :].bitcast(I32)
@@ -112,15 +112,17 @@ def tile_picked_yngcf_none_p_kernel(
             )
             nc.scalar.copy(out=h_sb[t][:, j0:j1], in_=h_ps[:])
 
-        w1_bf = [tile(f"w1_bf{a}", [P, 2, P * PACK], BF16) for a in range(2)]
-        for c in range(2):
-            deal(nc.vector.tensor_copy, w1_bf[0], w1_raw[c], cuts[c] // PACK, 0)
-            deal(nc.scalar.copy, w1_bf[1], w1_raw[c], cuts[c] // PACK, 2)
+        w1_turned = [tile(f"w1_turned{c}", [P, 2, P // 2 * PACK], BF16) for c in range(2)]
+        w1_straight = tile("w1_straight", [P, 2, P * PACK], BF16)
         w1_codes = tile("w1_codes", [P, H], U32)
         w1_sc = tile("w1_sc", [P, H], U8)
-        quantize(w1_codes[:, 0:P], w1_sc[:, 0:P], w1_bf[0][:, 0, :])
-        quantize(w1_codes[:, P : 2 * P], w1_sc[:, P : 2 * P], w1_bf[0][:, 1, :])
-        quantize(w1_codes[:, 2 * P :], w1_sc[:, 2 * P :], w1_bf[1][:].rearrange("p t c -> p (t c)"))
+        for c in range(2):
+            deal(nc.vector.tensor_copy, w1_turned[c], w1_raw[c], 0, 0)
+            deal(nc.scalar.copy, w1_straight, w1_raw[c], c * P // 2, 2)
+            quantize(
+                w1_codes[:, c * P : (c + 1) * P], w1_sc[:, c * P : (c + 1) * P], w1_turned[c][:].rearrange("p t c -> p (t c)")
+            )
+        quantize(w1_codes[:, 2 * P :], w1_sc[:, 2 * P :], w1_straight[:].rearrange("p t c -> p (t c)"))
         pieces = [(0, 0, S // 2), (0, S // 2, S)] + [(t, 0, S) for t in range(1, PACK)]
         for b, (t, j0, j1) in enumerate(pieces):
             h_piece(b, t, w1_codes[:, t * P : (t + 1) * P], w1_sc[:, t * P : (t + 1) * P], j0, j1)
@@ -155,12 +157,12 @@ def tile_picked_yngcf_none_p_kernel(
 
         for t in range(2):
             for d in range(2):
-                fetch(t == 0 or d == 1, picked[t][d][:], t, pos_sb[d][:])
+                fetch(True, picked[t][d][:], t, pos_sb[d][:])
                 for u in range(2):
                     nc.tensor.transpose(turned[d][:, u, t], picked[t][d][:, u * HALF : (u + 1) * HALF], ident[:])
         for e in range(2):
             fetch(False, by_first[:, e], 2 + e, pos_sb[0][:])
-        fetch(True, by_second[:], 2, pos_sb[1][:])
+        fetch(False, by_second[:], 2, pos_sb[1][:])
         fetch(False, last[1][:], 3, pos_sb[1][:, HALF // 16 :])
 
         gates = bank("gates", [P, 2, V], 7)
@@ -189,7 +191,8 @@ def tile_picked_yngcf_none_p_kernel(
         for u in range(2):
             for d in (1, 0):
                 nc.scalar.activation(
-                    out=scaled[u][:, d], in_=turned[d][:, u], func=COPY, scale=gate_col[:, 2 * d + u : 2 * d + u + 1]
+                    out=scaled[u][:, d].rearrange("v e (c m) -> v e c m", c=2),
+                    in_=turned[d][:, u].rearrange("v c (e m) -> v e c m", e=2), func=COPY, scale=gate_col[:, 2 * d + u : 2 * d + u + 1]
                 )
 
         def user_product(u):

@@ -74,7 +74,7 @@ def tile_picked_yngcf_none_p_kernel(
         nc.sync.dma_start(out=w1_raw[1][:], in_=w1_rows[:, :, H // 2 :])
         for q in range(4):
             nc.sync.dma_start(
-                out=es_tab[32 * q : 32 * q + 4, :].bitcast(I32), in_=e_scales[0, 4 * q : 4 * q + 4, :].bitcast(I32)
+                out=es_tab[q:P:32, :].bitcast(I32), in_=e_scales[0, q:16:4, :].bitcast(I32)
             )
         nc.sync.dma_start(out=w2_raw[0][:], in_=w2_rows[:, :, : cuts[1]])
         nc.sync.dma_start(pos_sb[0][:], pos1)

@@ -47,28 +47,28 @@ def tile_picked_yngcf_none_p_kernel(
         ew_tab = tile("ew_tab", [P, T], I32)
         gate_col = tile("gate_col", [P, 4], F32)
         cuts = (0, 3 * H // 4, H)
-        w1_raw = [tile(f"w1_raw{c}", [P, PACK, H // 2], F32) for c in range(2)]
+        w1_raw = [laid(f"w1_raw{c}", [P, PACK, H // 2], F32, (20480, 16384)[c]) for c in range(2)]
         w2_raw = [tile("w2_raw0", [P, PACK, cuts[1]], F32), laid("w2_raw1", [P, PACK, H - cuts[1]], F32, 3072)]
         w34_raw = [tile(f"w34_raw{s}", [P, PACK, N], F32) for s in range(2)]
         xs_tab = tile("xs_tab", [P, T], U8)
         es_tab = tile("es_tab", [P, T], U8)
         ident = tile("ident", [P, P], F32)
 
-        def load_words(tab, words):
-            nc.sync.dma_start(out=tab[:], in_=words[0].rearrange("p n t -> p (n t)").bitcast(I32))
+        def load_words(queue, tab, words):
+            queue.dma_start(out=tab[:], in_=words[0].rearrange("p n t -> p (n t)").bitcast(I32))
 
+        nc.gpsimd.memset(xs_tab[:].bitcast(I32), 0)
         nc.gpsimd.memset(es_tab[:].bitcast(I32), 0)
         make_identity(nc, ident[:])
         w1_rows = w1.rearrange("(p j) c -> p j c", j=PACK)
         w2_rows = w2.rearrange("(p j) c -> p j c", j=PACK)
 
         nc.sync.dma_start(offs_sb[:], offs)
+        load_words(nc.sync, xw_tab, x_words)
         for q in range(4):
             (nc.scalar, nc.sync)[q % 2].dma_start(
-                out=xs_tab[32 * q : 32 * q + 32, :].bitcast(I32),
-                in_=x_scales[0, 4 * q : 4 * q + 4, :].bitcast(I32).partition_broadcast(8),
+                out=xs_tab[q:P:32, :].bitcast(I32), in_=x_scales[0, q:16:4, :].bitcast(I32)
             )
-        load_words(xw_tab, x_words)
         nc.sync.dma_start(out=w1_raw[0][:], in_=w1_rows[:, :, : H // 2])
         nc.sync.dma_start(usr_sb[:], usr)
         nc.sync.dma_start(out=w1_raw[1][:], in_=w1_rows[:, :, H // 2 :])
@@ -82,15 +82,15 @@ def tile_picked_yngcf_none_p_kernel(
         gate_rows = gate.rearrange("d p (u v) -> (d p u) v", u=2)
         with nc.allow_non_contiguous_dma(reason="one gate value a partition"):
             nc.sync.dma_start(out=gate_col[:], in_=gate_rows[0:388:129, :].rearrange("n v -> v n"))
-        load_words(ew_tab, e_words)
+        load_words(nc.sync, ew_tab, e_words)
         nc.sync.dma_start(out=w2_raw[1][:], in_=w2_rows[:, :, cuts[1] :])
         for s, w in enumerate((w3, w4)):
             nc.sync.dma_start(out=w34_raw[s][:], in_=w.rearrange("(p j) c -> p j c", j=PACK))
 
         x_codes = tile("x_codes", [P, S], U32)
         x_sc = tile("x_sc", [P, S], U8)
-        nc.vector.tensor_copy(x_sc[:], xs_tab[:].indirect(offs_sb[:]))
         nc.vector.tensor_copy(x_codes[:], xw_tab[:].bitcast(U32).indirect(offs_sb[:]))
+        nc.vector.tensor_copy(x_sc[:], xs_tab[:].indirect(offs_sb[:]))
 
         def deal(copy, grouped, raw, m0, t0):
             n_t, n_m = grouped.shape[1], raw.shape[2] // PACK
@@ -102,7 +102,7 @@ def tile_picked_yngcf_none_p_kernel(
         def quantize(codes, scales, values):
             nc.vector.quantize_mx(out=codes.bitcast(FP8X4), scales=scales, in_=values)
 
-        h_sb = [tile(f"h_sb{t}", [P, S], F32) for t in range(PACK)]
+        h_sb = [laid("h_sb0", [P, S], F32, 16384)] + [tile(f"h_sb{t}", [P, S], F32) for t in range(1, PACK)]
 
         def h_piece(b, t, codes, scales, j0, j1):
             h_ps = bank(f"h_ps{b}", [P, j1 - j0], b)
@@ -112,12 +112,12 @@ def tile_picked_yngcf_none_p_kernel(
             )
             nc.scalar.copy(out=h_sb[t][:, j0:j1], in_=h_ps[:])
 
-        w1_turned = [tile(f"w1_turned{c}", [P, 2, P // 2 * PACK], BF16) for c in range(2)]
-        w1_straight = tile("w1_straight", [P, 2, P * PACK], BF16)
+        w1_turned = [tile("w1_turned0", [P, 2, P // 2 * PACK], BF16), laid("w1_turned1", [P, 2, P // 2 * PACK], BF16, 20480)]
+        w1_straight = laid("w1_straight", [P, 2, P * PACK], BF16, 8192 + 1024)
         w1_codes = tile("w1_codes", [P, H], U32)
         w1_sc = tile("w1_sc", [P, H], U8)
         for c in range(2):
-            deal(nc.vector.tensor_copy, w1_turned[c], w1_raw[c], 0, 0)
+            deal((nc.scalar.copy, nc.vector.tensor_copy)[c], w1_turned[c], w1_raw[c], 0, 0)
             deal(nc.scalar.copy, w1_straight, w1_raw[c], c * P // 2, 2)
             quantize(
                 w1_codes[:, c * P : (c + 1) * P], w1_sc[:, c * P : (c + 1) * P], w1_turned[c][:].rearrange("p t c -> p (t c)")

@@ -123,8 +123,8 @@ def tile_picked_yngcf_none_p_kernel(
                 w1_codes[:, c * P : (c + 1) * P], w1_sc[:, c * P : (c + 1) * P], w1_turned[c][:].rearrange("p t c -> p (t c)")
             )
         quantize(w1_codes[:, 2 * P :], w1_sc[:, 2 * P :], w1_straight[:].rearrange("p t c -> p (t c)"))
-        pieces = [(0, 0, S // 2), (0, S // 2, S)] + [(t, 0, S) for t in range(1, PACK)]
-        for b, (t, j0, j1) in enumerate(pieces):
+        pieces = [(t, j0, j0 + S // 2) for t in range(PACK) for j0 in (0, S // 2)]
+        for b, (t, j0, j1) in zip((0, 1, 2, 5, 3, 6, 4, 7), pieces):
             h_piece(b, t, w1_codes[:, t * P : (t + 1) * P], w1_sc[:, t * P : (t + 1) * P], j0, j1)
 
         e_codes = tile("e_codes", [P, V], U32)

@@ -79,11 +79,11 @@ def tile_picked_yngcf_none_p_kernel(
         nc.sync.dma_start(out=w2_raw[0][:], in_=w2_rows[:, :, : cuts[1]])
         nc.sync.dma_start(pos_sb[0][:], pos1)
         nc.sync.dma_start(pos_sb[1][:], pos2)
+        load_words(nc.sync, ew_tab, e_words)
+        nc.sync.dma_start(out=w2_raw[1][:], in_=w2_rows[:, :, cuts[1] :])
         gate_rows = gate.rearrange("d p (u v) -> (d p u) v", u=2)
         with nc.allow_non_contiguous_dma(reason="one gate value a partition"):
             nc.sync.dma_start(out=gate_col[:], in_=gate_rows[0:388:129, :].rearrange("n v -> v n"))
-        load_words(nc.sync, ew_tab, e_words)
-        nc.sync.dma_start(out=w2_raw[1][:], in_=w2_rows[:, :, cuts[1] :])
         for s, w in enumerate((w3, w4)):
             nc.sync.dma_start(out=w34_raw[s][:], in_=w.rearrange("(p j) c -> p j c", j=PACK))
 
@@ -99,6 +99,9 @@ def tile_picked_yngcf_none_p_kernel(
                 in_=raw[:].rearrange("p j (m t) -> p m j t", t=PACK)[:, :, :, t0 : t0 + n_t],
             )
 
+        def pool_deal(grouped, raw):
+            nc.gpsimd.tensor_scalar(grouped, raw, 1.0, 0.0, MULT, ADD)
+
         def quantize(codes, scales, values):
             nc.vector.quantize_mx(out=codes.bitcast(FP8X4), scales=scales, in_=values)
 
@@ -112,13 +115,19 @@ def tile_picked_yngcf_none_p_kernel(
             )
             nc.scalar.copy(out=h_sb[t][:, j0:j1], in_=h_ps[:])
 
-        w1_turned = [tile("w1_turned0", [P, 2, P // 2 * PACK], BF16), laid("w1_turned1", [P, 2, P // 2 * PACK], BF16, 20480)]
+        w1_turned = [laid("w1_turned0", [P, 2, P // 2 * PACK], BF16, 24576), laid("w1_turned1", [P, 2, P // 2 * PACK], BF16, 24576)]
         w1_straight = laid("w1_straight", [P, 2, P * PACK], BF16, 8192 + 1024)
         w1_codes = tile("w1_codes", [P, H], U32)
         w1_sc = tile("w1_sc", [P, H], U8)
         for c in range(2):
             deal((nc.scalar.copy, nc.vector.tensor_copy)[c], w1_turned[c], w1_raw[c], 0, 0)
-            deal(nc.scalar.copy, w1_straight, w1_raw[c], c * P // 2, 2)
+            if c == 0:
+                pool_deal(
+                    w1_straight[:].rearrange("p t (m j) -> p m t j", j=PACK)[:, : P // 2],
+                    w1_raw[0][:].rearrange("p j (m t) -> p m t j", t=PACK)[:, :, 2:],
+                )
+            else:
+                deal(nc.scalar.copy, w1_straight, w1_raw[c], P // 2, 2)
             quantize(
                 w1_codes[:, c * P : (c + 1) * P], w1_sc[:, c * P : (c + 1) * P], w1_turned[c][:].rearrange("p t c -> p (t c)")
             )
@@ -131,9 +140,6 @@ def tile_picked_yngcf_none_p_kernel(
         e_sc = tile("e_sc", [P, V], U8)
         nc.vector.tensor_copy(e_sc[:], es_tab[:].indirect(usr_sb[:]))
 
-
-        def pool_deal(grouped, raw):
-            nc.gpsimd.tensor_scalar(grouped, raw, 1.0, 0.0, MULT, ADD)
 
         w2_bf = laid("w2_bf", [P, PACK, P * PACK], BF16, 8192 + 1024)
         for c in range(2):

@@ -69,15 +69,15 @@ def tile_picked_yngcf_none_p_kernel(
             (nc.scalar, nc.sync)[q % 2].dma_start(
                 out=xs_tab[q:P:32, :].bitcast(I32), in_=x_scales[0, q:16:4, :].bitcast(I32)
             )
-        nc.sync.dma_start(out=w1_raw[0][:], in_=w1_rows[:, :, : H // 2])
         nc.sync.dma_start(usr_sb[:], usr)
+        nc.sync.dma_start(out=w1_raw[0][:], in_=w1_rows[:, :, : H // 2])
         nc.sync.dma_start(out=w1_raw[1][:], in_=w1_rows[:, :, H // 2 :])
         for q in range(4):
             nc.sync.dma_start(
                 out=es_tab[q:P:32, :].bitcast(I32), in_=e_scales[0, q:16:4, :].bitcast(I32)
             )
-        nc.sync.dma_start(out=w2_raw[0][:], in_=w2_rows[:, :, : cuts[1]])
         nc.sync.dma_start(pos_sb[0][:], pos1)
+        nc.sync.dma_start(out=w2_raw[0][:], in_=w2_rows[:, :, : cuts[1]])
         nc.sync.dma_start(pos_sb[1][:], pos2)
         load_words(nc.sync, ew_tab, e_words)
         nc.sync.dma_start(out=w2_raw[1][:], in_=w2_rows[:, :, cuts[1] :])
@@ -115,10 +115,10 @@ def tile_picked_yngcf_none_p_kernel(
             )
             nc.scalar.copy(out=h_sb[t][:, j0:j1], in_=h_ps[:])
 
-        w1_turned = [laid("w1_turned0", [P, 2, P // 2 * PACK], BF16, 24576), laid("w1_turned1", [P, 2, P // 2 * PACK], BF16, 24576)]
+        w1_turned = [laid("w1_turned0", [P, 2, P // 2 * PACK], BF16, 24576), laid("w1_turned1", [P, 2, P // 2 * PACK], BF16, 20480)]
         w1_straight = laid("w1_straight", [P, 2, P * PACK], BF16, 8192 + 1024)
         w1_codes = tile("w1_codes", [P, H], U32)
-        w1_sc = tile("w1_sc", [P, H], U8)
+        w1_sc = [tile("w1_sc0", [P, 2 * P], U8), laid("w1_sc1", [P, 2 * P], U8, 16384 + 2048)]
         for c in range(2):
             deal((nc.scalar.copy, nc.vector.tensor_copy)[c], w1_turned[c], w1_raw[c], 0, 0)
             if c == 0:
@@ -129,12 +129,12 @@ def tile_picked_yngcf_none_p_kernel(
             else:
                 deal(nc.scalar.copy, w1_straight, w1_raw[c], P // 2, 2)
             quantize(
-                w1_codes[:, c * P : (c + 1) * P], w1_sc[:, c * P : (c + 1) * P], w1_turned[c][:].rearrange("p t c -> p (t c)")
+                w1_codes[:, c * P : (c + 1) * P], w1_sc[0][:, c * P : (c + 1) * P], w1_turned[c][:].rearrange("p t c -> p (t c)")
             )
-        quantize(w1_codes[:, 2 * P :], w1_sc[:, 2 * P :], w1_straight[:].rearrange("p t c -> p (t c)"))
+        quantize(w1_codes[:, 2 * P :], w1_sc[1][:], w1_straight[:].rearrange("p t c -> p (t c)"))
         pieces = [(t, j0, j0 + S // 2) for t in range(PACK) for j0 in (0, S // 2)]
         for b, (t, j0, j1) in zip((0, 1, 2, 5, 3, 6, 4, 7), pieces):
-            h_piece(b, t, w1_codes[:, t * P : (t + 1) * P], w1_sc[:, t * P : (t + 1) * P], j0, j1)
+            h_piece(b, t, w1_codes[:, t * P : (t + 1) * P], w1_sc[t // 2][:, t % 2 * P : (t % 2 + 1) * P], j0, j1)
 
         e_codes = tile("e_codes", [P, V], U32)
         e_sc = tile("e_sc", [P, V], U8)
@@ -151,7 +151,7 @@ def tile_picked_yngcf_none_p_kernel(
         picked = [[tile(f"picked{t}{d}", [P, V], F32) for d in range(2)] for t in range(2)]
         by_first = tile("by_first", [P, 2, V], F32)
         by_second = tile("by_second", [P, V], F32)
-        last = [laid("last0", [P, HALF], F32, 3136), tile("last1", [P, HALF], F32)]
+        last = [laid("last0", [P, HALF], F32, 3136), laid("last1", [P, HALF], F32, 3648)]
         turned = [bank(f"turned{d}", [P, 2, 2, P], 5 + d) for d in range(2)]
 
         def fetch(on_vector, dst, t, offsets):
@@ -169,7 +169,6 @@ def tile_picked_yngcf_none_p_kernel(
         for e in range(2):
             fetch(False, by_first[:, e], 2 + e, pos_sb[0][:])
         fetch(False, by_second[:], 2, pos_sb[1][:])
-        fetch(False, last[1][:], 3, pos_sb[1][:, HALF // 16 :])
 
         gates = bank("gates", [P, 2, V], 7)
         for d in range(2):
@@ -200,6 +199,8 @@ def tile_picked_yngcf_none_p_kernel(
                     out=scaled[u][:, d].rearrange("v e (c m) -> v e c m", c=2),
                     in_=turned[d][:, u].rearrange("v c (e m) -> v e c m", e=2), func=COPY, scale=gate_col[:, 2 * d + u : 2 * d + u + 1]
                 )
+            if u == 0:
+                fetch(False, last[1][:], 3, pos_sb[1][:, HALF // 16 :])
 
         def user_product(u):
             gg_ps.append(bank(f"gg_ps{u}", [P, PACK, HALF], (2, 5)[u]))

from contextlib import ExitStack

import concourse.mybir as mybir
from concourse.masks import make_identity

K, T, S, V, H, N = 512, 1024, 512, 256, 512, 128
FLOPS = 2 * K * H * S + 2 * K * H * V + 2 * 2 * H * N * V

F32 = mybir.dt.float32
BF16 = mybir.dt.bfloat16
I32 = mybir.dt.int32
U32 = mybir.dt.uint32
U16 = mybir.dt.uint16
U8 = mybir.dt.uint8
FP8X4 = mybir.dt.float8_e4m3fn_x4
MULT = mybir.AluOpType.mult
ADD = mybir.AluOpType.add
COPY = mybir.ActivationFunctionType.Copy

P = 128
PACK = 4
HALF = V // 2


def tile_picked_yngcf_none_p_kernel(
    tc, x_words, x_scales, e_words, e_scales, w1, w2, w3, w4, gate, offs, usr, pos1, pos2, out
):
    nc = tc.nc
    with ExitStack() as ctx:
        sb = ctx.enter_context(tc.tile_pool(name="sb", bufs=1))
        shared = ctx.enter_context(tc.tile_pool(name="shared", bufs=1))
        ps = ctx.enter_context(tc.psum_pool(name="ps", bufs=1))

        def tile(name, shape, dtype, tag=None):
            return sb.tile(shape, dtype, name=name, tag=tag or name, align_bytes=64)

        def laid(name, shape, dtype, offset):
            return shared.tile(shape, dtype, name=name, tag=name, align_bytes=64, offset=offset)

        def bank(name, shape, b):
            return ps.tile(shape, F32, name=name, tag=f"bank{b}")

        offs_sb = tile("offs_sb", [P, S // 16], U16)
        usr_sb = tile("usr_sb", [P, V // 16], U16)
        pos_sb = [tile(f"pos_sb{d}", [P, V // 16], U16) for d in range(2)]
        xw_tab = tile("xw_tab", [P, T], I32)
        ew_tab = tile("ew_tab", [P, T], I32)
        gate_col = tile("gate_col", [P, 4], F32)
        cuts = (0, 3 * H // 4, H)
        w1_raw = [laid(f"w1_raw{c}", [P, PACK, H // 2], F32, (20480, 16384)[c]) for c in range(2)]
        w2_raw = [tile("w2_raw0", [P, PACK, cuts[1]], F32), laid("w2_raw1", [P, PACK, H - cuts[1]], F32, 3072)]
        w34_raw = [tile(f"w34_raw{s}", [P, PACK, N], F32) for s in range(2)]
        xs_tab = tile("xs_tab", [P, T], U8)
        es_tab = tile("es_tab", [P, T], U8)
        ident = tile("ident", [P, P], F32)

        def load_words(queue, tab, words):
            queue.dma_start(out=tab[:], in_=words[0].rearrange("p n t -> p (n t)").bitcast(I32))

        nc.gpsimd.memset(xs_tab[:].bitcast(I32), 0)
        nc.gpsimd.memset(es_tab[:].bitcast(I32), 0)
        make_identity(nc, ident[:])
        w1_rows = w1.rearrange("(p j) c -> p j c", j=PACK)
        w2_rows = w2.rearrange("(p j) c -> p j c", j=PACK)

        nc.sync.dma_start(offs_sb[:], offs)
        load_words(nc.sync, xw_tab, x_words)
        for q in range(4):
            (nc.scalar, nc.sync)[q % 2].dma_start(
                out=xs_tab[q:P:32, :].bitcast(I32), in_=x_scales[0, q:16:4, :].bitcast(I32)
            )
        nc.sync.dma_start(usr_sb[:], usr)
        nc.sync.dma_start(out=w1_raw[0][:], in_=w1_rows[:, :, : H // 2])
        nc.sync.dma_start(out=w1_raw[1][:], in_=w1_rows[:, :, H // 2 :])
        for q in range(4):
            nc.sync.dma_start(
                out=es_tab[q:P:32, :].bitcast(I32), in_=e_scales[0, q:16:4, :].bitcast(I32)
            )
        nc.sync.dma_start(pos_sb[0][:], pos1)
        nc.sync.dma_start(out=w2_raw[0][:], in_=w2_rows[:, :, : cuts[1]])
        nc.sync.dma_start(pos_sb[1][:], pos2)
        load_words(nc.sync, ew_tab, e_words)
        nc.sync.dma_start(out=w2_raw[1][:], in_=w2_rows[:, :, cuts[1] :])
        gate_rows = gate.rearrange("d p (u v) -> (d p u) v", u=2)
        with nc.allow_non_contiguous_dma(reason="one gate value a partition"):
            nc.sync.dma_start(out=gate_col[:], in_=gate_rows[0:388:129, :].rearrange("n v -> v n"))
        for s, w in enumerate((w3, w4)):
            nc.sync.dma_start(out=w34_raw[s][:], in_=w.rearrange("(p j) c -> p j c", j=PACK))

        x_codes = tile("x_codes", [P, S], U32)
        x_sc = tile("x_sc", [P, S], U8)
        nc.vector.tensor_copy(x_codes[:], xw_tab[:].bitcast(U32).indirect(offs_sb[:]))
        nc.vector.tensor_copy(x_sc[:], xs_tab[:].indirect(offs_sb[:]))

        def deal(copy, grouped, raw, m0, t0):
            n_t, n_m = grouped.shape[1], raw.shape[2] // PACK
            copy(
                out=grouped[:].rearrange("p t (m j) -> p m j t", j=PACK)[:, m0 : m0 + n_m],
                in_=raw[:].rearrange("p j (m t) -> p m j t", t=PACK)[:, :, :, t0 : t0 + n_t],
            )

        def pool_deal(grouped, raw):
            nc.gpsimd.tensor_scalar(grouped, raw, 1.0, 0.0, MULT, ADD)

        def quantize(codes, scales, values):
            nc.vector.quantize_mx(out=codes.bitcast(FP8X4), scales=scales, in_=values)

        h_sb = [laid("h_sb0", [P, S], F32, 16384)] + [tile(f"h_sb{t}", [P, S], F32) for t in range(1, PACK)]

        def h_piece(b, t, codes, scales, j0, j1):
            h_ps = bank(f"h_ps{b}", [P, j1 - j0], b)
            nc.tensor.matmul_mx(
                out=h_ps[:], lhsT=codes.bitcast(FP8X4), lhsT_scale=scales,
                rhs=x_codes[:, j0:j1].bitcast(FP8X4), rhs_scale=x_sc[:, j0:j1], start=True, stop=True,
            )
            nc.scalar.copy(out=h_sb[t][:, j0:j1], in_=h_ps[:])

        w1_turned = [laid("w1_turned0", [P, 2, P // 2 * PACK], BF16, 24576), laid("w1_turned1", [P, 2, P // 2 * PACK], BF16, 20480)]
        w1_straight = laid("w1_straight", [P, 2, P * PACK], BF16, 8192 + 1024)
        w1_codes = tile("w1_codes", [P, H], U32)
        w1_sc = [tile("w1_sc0", [P, 2 * P], U8), laid("w1_sc1", [P, 2 * P], U8, 16384 + 2048)]
        for c in range(2):
            deal((nc.scalar.copy, nc.vector.tensor_copy)[c], w1_turned[c], w1_raw[c], 0, 0)
            if c == 0:
                pool_deal(
                    w1_straight[:].rearrange("p t (m j) -> p m t j", j=PACK)[:, : P // 2],
                    w1_raw[0][:].rearrange("p j (m t) -> p m t j", t=PACK)[:, :, 2:],
                )
            else:
                deal(nc.scalar.copy, w1_straight, w1_raw[c], P // 2, 2)
            quantize(
                w1_codes[:, c * P : (c + 1) * P], w1_sc[0][:, c * P : (c + 1) * P], w1_turned[c][:].rearrange("p t c -> p (t c)")
            )
        quantize(w1_codes[:, 2 * P :], w1_sc[1][:], w1_straight[:].rearrange("p t c -> p (t c)"))
        pieces = [(t, j0, j0 + S // 2) for t in range(PACK) for j0 in (0, S // 2)]
        for b, (t, j0, j1) in zip((0, 1, 2, 5, 3, 6, 4, 7), pieces):
            h_piece(b, t, w1_codes[:, t * P : (t + 1) * P], w1_sc[t // 2][:, t % 2 * P : (t % 2 + 1) * P], j0, j1)

        e_codes = tile("e_codes", [P, V], U32)
        e_sc = tile("e_sc", [P, V], U8)
        nc.vector.tensor_copy(e_sc[:], es_tab[:].indirect(usr_sb[:]))


        w2_bf = laid("w2_bf", [P, PACK, P * PACK], BF16, 8192 + 1024)
        for c in range(2):
            pool_deal(
                w2_bf[:].rearrange("p t (m j) -> p m t j", j=PACK)[:, cuts[c] // PACK : cuts[c + 1] // PACK],
                w2_raw[c][:].rearrange("p j (m t) -> p m t j", t=PACK),
            )

        picked = [[tile(f"picked{t}{d}", [P, V], F32) for d in range(2)] for t in range(2)]
        by_first = tile("by_first", [P, 2, V], F32)
        by_second = tile("by_second", [P, V], F32)
        last = [laid("last0", [P, HALF], F32, 3136), laid("last1", [P, HALF], F32, 3648)]
        turned = [bank(f"turned{d}", [P, 2, 2, P], 5 + d) for d in range(2)]

        def fetch(on_vector, dst, t, offsets):
            src = h_sb[t][:].indirect(offsets)
            if on_vector:
                nc.vector.tensor_copy(dst, src)
            else:
                nc.scalar.activation(out=dst, in_=src, func=COPY)

        for t in range(2):
            for d in range(2):
                fetch(True, picked[t][d][:], t, pos_sb[d][:])
                for u in range(2):
                    nc.tensor.transpose(turned[d][:, u, t], picked[t][d][:, u * HALF : (u + 1) * HALF], ident[:])
        for e in range(2):
            fetch(False, by_first[:, e], 2 + e, pos_sb[0][:])
        fetch(False, by_second[:], 2, pos_sb[1][:])

        gates = bank("gates", [P, 2, V], 7)
        for d in range(2):
            for u in range(2):
                nc.tensor.transpose(
                    gates[:, d, u * HALF : (u + 1) * HALF],
                    gate_col[:, 2 * d + u : 2 * d + u + 1].to_broadcast([P, P]), ident[:],
                )

        nc.vector.tensor_copy(e_codes[:], ew_tab[:].bitcast(U32).indirect(usr_sb[:]))
        w2_codes = tile("w2_codes", [P, H], U32)
        w2_sc = tile("w2_sc", [P, H], U8)
        quantize(w2_codes[:], w2_sc[:], w2_bf[:].rearrange("p t c -> p (t c)"))
        fetch(True, last[0][:], 3, pos_sb[1][:, : HALF // 16])
        w34_bf = laid("w34_bf", [P, 2, N * PACK], BF16, 8192 + 4096)
        pool_deal(w34_bf[:, 0].rearrange("p (c j) -> p c j", j=PACK), w34_raw[0][:].rearrange("p j c -> p c j"))
        pool_deal(
            w34_bf[:, 1].rearrange("p (c j) -> p c j", j=PACK)[:, : N // 4], w34_raw[1][:].rearrange("p j c -> p c j")[:, : N // 4]
        )

        scaled = [laid(f"scaled{u}", [P, 2, 2, P], F32, (1088, 4160)[u]) for u in range(2)]
        terms = laid("terms", [P, 2, 2, V], F32, 8192)
        z = [tile(f"z{u}", [P, PACK, HALF], F32) for u in range(2)]
        gg_ps, z01_ps = [], []
        for u in range(2):
            for d in (1, 0):
                nc.scalar.activation(
                    out=scaled[u][:, d].rearrange("v e (c m) -> v e c m", c=2),
                    in_=turned[d][:, u].rearrange("v c (e m) -> v e c m", e=2), func=COPY, scale=gate_col[:, 2 * d + u : 2 * d + u + 1]
                )
            if u == 0:
                fetch(False, last[1][:], 3, pos_sb[1][:, HALF // 16 :])

        def user_product(u):
            gg_ps.append(bank(f"gg_ps{u}", [P, PACK, HALF], (2, 5)[u]))
            for t in range(PACK):
                nc.tensor.matmul_mx(
                    out=gg_ps[u][:, t, :], lhsT=w2_codes[:, t * P : (t + 1) * P].bitcast(FP8X4),
                    lhsT_scale=w2_sc[:, t * P : (t + 1) * P],
                    rhs=e_codes[:, u * HALF : (u + 1) * HALF].bitcast(FP8X4),
                    rhs_scale=e_sc[:, u * HALF : (u + 1) * HALF], start=True, stop=True,
                )

        user_product(0)
        for u in range(2):
            z01_ps.append(bank(f"z01_ps{u}", [P, 2, HALF], u))
            passes = [(d, e) for d in (1, 0) for e in range(2)] if u else [(d, e) for e in range(2) for d in range(2)]
            for d, e in passes:
                nc.tensor.matmul(
                    z01_ps[u][:, e], lhsT=scaled[u][:, d, e], rhs=ident[:], is_transpose=True,
                    start=(d, e) == (1, 0) if u else d == 0, stop=(d, e) == (0, 1) if u else d == 1,
                )
        user_product(1)
        nc.vector.tensor_tensor(terms[:, 1, 0], by_second[:], gates[:, 1], MULT)
        nc.vector.tensor_tensor(terms[:, 1, 1, :HALF], last[0][:], gates[:, 1, :HALF], MULT)
        for u in range(2):
            users = slice(u * HALF, (u + 1) * HALF)
            nc.vector.tensor_tensor(
                terms[:, 0, :, users], by_first[:, :, users], gates[:, 0, users].unsqueeze(1).to_broadcast([P, 2, HALF]), MULT
            )
        nc.vector.tensor_tensor(terms[:, 1, 1, HALF:], last[1][:], gates[:, 1, HALF:], MULT)
        for u in range(2):
            users = slice(u * HALF, (u + 1) * HALF)
            nc.vector.tensor_tensor(z[u][:, 2:4], terms[:, 0, :, users], terms[:, 1, :, users], ADD)
            nc.scalar.copy(out=z[u][:, 0:2], in_=z01_ps[u][:])
            if u == 0:
                nc.scalar.copy(
                    out=w34_bf[:, 1].rearrange("p (c i j) -> p c j i", i=4, j=PACK)[:, N // 16 :],
                    in_=w34_raw[1][:].rearrange("p j (c i) -> p c j i", i=4)[:, N // 16 :],
                )

        zy_bf = [
            [laid("z0_bf", [P, HALF * PACK], BF16, 8192), tile("y0_bf", [P, HALF * PACK], BF16)],
            [tile("z1_bf", [P, HALF * PACK], BF16), tile("y1_bf", [P, HALF * PACK], BF16)],
        ]
        for u in range(2):
            z_walk = z[u][:].rearrange("p t (c i) -> p c t i", i=4)
            if u == 0:
                pool_deal(zy_bf[u][0][:].rearrange("p (c t) -> p c t", t=PACK), z[u][:].rearrange("p t c -> p c t"))
            else:
                nc.scalar.copy(out=zy_bf[u][0][:].rearrange("p (c i t) -> p c t i", i=4, t=PACK), in_=z_walk)
            nc.vector.tensor_tensor(
                zy_bf[u][1][:].rearrange("p (c i t) -> p c t i", i=4, t=PACK),
                gg_ps[u][:].rearrange("p t (c i) -> p c t i", i=4), z_walk, MULT,
            )
        w34_codes = tile("w34_codes", [P, 2 * N], U32, "z0")
        w34_sc = tile("w34_sc", [P, 2 * N], U8)
        quantize(w34_codes[:], w34_sc[:], w34_bf[:].rearrange("p s c -> p (s c)"))
        for u in range(2):
            zy_codes = tile(f"zy_codes{u}", [P, 2 * HALF], U32)
            zy_sc = tile(f"zy_sc{u}", [P, 2 * HALF], U8)
            out_ps = bank(f"out_ps{u}", [P, HALF], 3 + u)
            for s in range(2):
                cols = slice(s * HALF, (s + 1) * HALF)
                quantize(zy_codes[:, cols], zy_sc[:, cols], zy_bf[u][s][:])
                nc.tensor.matmul_mx(
                    out=out_ps[:], lhsT=w34_codes[:, s * N : (s + 1) * N].bitcast(FP8X4),
                    lhsT_scale=w34_sc[:, s * N : (s + 1) * N],
                    rhs=zy_codes[:, cols].bitcast(FP8X4), rhs_scale=zy_sc[:, cols], start=(s == 0), stop=(s == 1),
                )
            out_sb = tile(f"out_sb{u}", [P, HALF], F32)
            nc.scalar.copy(out=out_sb[:], in_=out_ps[:])
            (nc.sync, nc.scalar)[u].dma_start(out=out[:, u * HALF : (u + 1) * HALF], in_=out_sb[:])
